import numpy as np
import ml_dtypes


def mxq(x, axis, fmt="e4m3"):
    dtype, down = {"e4m3": (ml_dtypes.float8_e4m3fn, 7), "e5m2": (ml_dtypes.float8_e5m2, 14)}[fmt]
    v = np.moveaxis(np.asarray(x, np.float32).astype(ml_dtypes.bfloat16).astype(np.float64), axis, -1)
    blocks = v.reshape(v.shape[:-1] + (-1, 32))
    amax = np.abs(blocks).max(-1, keepdims=True)
    byte = np.maximum(np.where(amax > 0, np.frexp(amax)[1] - 1 + 127, 0) - down, 1)
    scale = np.exp2(byte - 127.0)
    codes = (blocks / scale).astype(np.float32).astype(dtype).astype(np.float64)
    return np.moveaxis((codes * scale).reshape(v.shape), -1, axis)


WIDE = False


def mx_kscale(k):
    if not WIDE:
        return np.ones(k)
    levels = np.array([10, -10, 5, -5, 0])
    if k % 512:
        return np.exp2(np.random.permutation(np.resize(levels, k // 32))).repeat(32)
    a = np.empty((k // 512, 16))
    for p in range(k // 512):
        a[p, :8] = np.random.permutation(np.resize(levels, 8))
        for g in range(8):
            far = levels[np.abs(levels - a[p, g]) >= 10]
            a[p, g + 8] = far[np.random.randint(len(far))]
    return np.exp2(a.ravel()).repeat(32)


def f64(x):
    return np.asarray(x).astype(np.float64)


def striped(idx):
    return np.tile(idx.reshape(-1, 16).T, (8, 1)).astype(np.uint16)


def unstriped(offs):
    return offs[:16].T.reshape(-1).astype(np.int64)


def pack_weight(w):
    k, n = w.shape
    w = f64(np.asarray(w, np.float32).astype(ml_dtypes.bfloat16)).reshape(k // 32, 32, n)
    amax = np.abs(w).max(1)
    byte = np.clip(np.where(amax > 0, np.frexp(amax)[1] - 1 + 127 - 7, 1), 1, 254)
    scaled = (w * np.exp2(127.0 - byte)[:, None, :]).reshape(k, n).astype(np.float32)
    words = np.ascontiguousarray(scaled.reshape(k // 512, 128, 4, n).transpose(0, 1, 3, 2)).astype(ml_dtypes.float8_e4m3fn).view(np.uint8)
    return words, np.ascontiguousarray(byte.astype(np.uint8).reshape(k // 512, 16, n))


def unpack_weight(words, scales):
    g, p, n, _ = words.shape
    vals = np.ascontiguousarray(words).view(ml_dtypes.float8_e4m3fn).astype(np.float64) * np.repeat(np.exp2(scales.astype(np.float64) - 127.0), 8, axis=1)[..., None]
    return vals.transpose(0, 1, 3, 2).reshape(g * 512, n)


def planes(y):
    n, m = y.shape
    v = y.astype(np.float32).astype(ml_dtypes.bfloat16).astype(np.float64).reshape(n // 32, 32, m)
    top = np.abs(v).max(1)
    byte = np.clip(np.where(top > 0, np.frexp(top)[1] - 1 + 127 - 7, 1), 1, 254)
    codes = (v * np.exp2(127.0 - byte)[:, None, :]).reshape(n, m).astype(np.float32).astype(ml_dtypes.float8_e4m3fn).view(np.uint8)
    words = codes.reshape(n // 512, 128, 4, m).transpose(0, 1, 3, 2)
    return np.ascontiguousarray(words), np.ascontiguousarray(byte.astype(np.uint8).reshape(n // 512, 16, m))


K, T, S, D, V, H, N = 1024, 1024, 512, 2, 256, 512, 512
P = 2 ** 7


def setup_inputs():
    n = np.random.standard_normal
    s = mx_kscale(K)[:, None]
    u = mx_kscale(H)
    near = np.random.permutation(S)
    packed_xT = pack_weight(n((K, T)) * s)
    return {
        "x_words": packed_xT[0],
        "x_scales": packed_xT[1],
        "w1": (n((K, H)) / np.sqrt(K) / s * u).astype(np.float32),
        "w2": (n((H, N)) / np.sqrt(H) / u[:, None]).astype(np.float32),
        "gate": (np.tile(np.random.uniform(0.1, 0.6, (D, 1, V)), (1, P, 1))).astype(np.float32),
        "ref": (n((H, V)) * u[:, None]).astype(np.float32),
        "offs": striped(np.random.permutation(T)[:S]),
        "pos1": striped(near[:V]),
        "pos2": striped(near[V:]),
    }


def reference(x_words, x_scales, w1, w2, gate, ref, offs, pos1, pos2):
    xq = unpack_weight(x_words, x_scales)[:, unstriped(offs)]
    f = mxq(f64(w1), 0, "e4m3").T @ xq
    e = f64(ref) - (f[:, unstriped(pos1)] * f64(gate)[0, :1] + f[:, unstriped(pos2)] * f64(gate)[1, :1])
    z = np.abs(e)
    out_0 = mxq(f64(w2), 0, "e4m3").T @ mxq(z, 0, "e4m3")
    return (out_0,) + planes(out_0)

@@ -1,0 +1,212 @@
+from contextlib import ExitStack
+
+import concourse.mybir as mybir
+from concourse.masks import make_identity
+
+F32 = mybir.dt.float32
+BF16 = mybir.dt.bfloat16
+I32 = mybir.dt.int32
+U32 = mybir.dt.uint32
+U16 = mybir.dt.uint16
+U8 = mybir.dt.uint8
+FP8X4 = mybir.dt.float8_e4m3fn_x4
+MULT = mybir.AluOpType.mult
+ACT = mybir.ActivationFunctionType
+
+P = 128
+K, T, S, V, H, N = 1024, 1024, 512, 256, 512, 512
+FLOPS = 2 * K * H * S + 2 * H * N * V
+
+
+def tile_picked_zwarp_abs_po_kernel(
+    tc, x_words, x_scales, w1, w2, gate, ref, offs, pos1, pos2, out_0, out_1, out_2
+):
+    nc = tc.nc
+    with ExitStack() as ctx:
+        lists = ctx.enter_context(tc.tile_pool(name="lists", bufs=1))
+        sb = ctx.enter_context(tc.tile_pool(name="sb", bufs=1))
+        overlay = ctx.enter_context(tc.tile_pool(name="overlay", bufs=1))
+        psum = ctx.enter_context(tc.psum_pool(name="psum", bufs=1))
+        banks = [psum.tile([P, 512], F32, name="bank%d" % b) for b in range(8)]
+
+        def tile(shape, dtype, name):
+            return sb.tile(shape, dtype, name=name, align_bytes=64)
+
+        ident = tile([P, P], F32, "ident")
+        make_identity(nc, ident[:])
+
+        offs_sb = lists.tile([P, S // 16], U16, name="offs_sb")
+        pos_sb = [lists.tile([P, V // 16], U16, name="pos_sb%d" % d) for d in range(2)]
+        nc.sync.dma_start(offs_sb[:], offs)
+
+        xs_all = tile([P, T], U8, "xs_all")
+        nc.vector.memset(xs_all[:].bitcast(I32), 0)
+        for q in range(4):
+            nc.scalar.dma_start(xs_all[32 * q : 32 * q + 8, :].bitcast(I32), x_scales[:, 4 * q : 4 * q + 4, :].bitcast(I32))
+
+        xw_all = [tile([P, T], I32, "xw_all%d" % o) for o in range(2)]
+        for o in range(2):
+            nc.sync.dma_start(xw_all[o][:], x_words[o].rearrange("p c r -> p (c r)").bitcast(I32))
+
+        w1_raw = {}
+
+        def load_w1(c, chunks, o):
+            raw = tile([P, 4, P * chunks], F32, "w1_raw%d%d" % (c, o))
+            rows = w1[512 * o : 512 * (o + 1), P * c : P * (c + chunks)]
+            nc.sync.dma_start(raw[:], rows.rearrange("(p j) c -> p j c", j=4))
+            w1_raw[c, o] = raw
+
+        load_w1(0, 1, 0)
+        load_w1(0, 1, 1)
+        gate_sb = tile([P, 2, V], F32, "gate_sb")
+        nc.sync.dma_start(gate_sb[:], gate.rearrange("d p v -> p d v"))
+        load_w1(1, 1, 0)
+        load_w1(1, 1, 1)
+        nc.sync.dma_start(pos_sb[0][:], pos1)
+        nc.sync.dma_start(pos_sb[1][:], pos2)
+        load_w1(2, 2, 0)
+        load_w1(2, 2, 1)
+        ref_sb = tile([P, 4, V], F32, "ref_sb")
+        nc.sync.dma_start(ref_sb[:], ref.rearrange("(c p) v -> p c v", p=P))
+        w2_raw = tile([P, 4, N], F32, "w2_raw")
+        nc.sync.dma_start(w2_raw[:], w2.rearrange("(p j) m -> p j m", j=4))
+
+        warm = tile([P, 1], F32, "warm")
+        nc.scalar.activation(warm[:], ident[:, 0:1], ACT.Abs)
+
+        xs = tile([P, S], U8, "xs")
+        xw = [tile([P, S], U32, "xw%d" % o) for o in range(2)]
+
+        def pick_words(o, cols):
+            offsets = offs_sb[:, cols.start // 16 : cols.stop // 16]
+            nc.vector.tensor_copy(xw[o][:, cols], xw_all[o][:].bitcast(U32).indirect(offsets))
+
+        pick_words(0, slice(0, S))
+        nc.vector.tensor_copy(xs[:], xs_all[:].indirect(offs_sb[:]))
+
+        w1_q = {}
+        twice_bf = tile([P, P, 4], BF16, "twice_bf")
+        last_bf = tile([P, N, 4], BF16, "last_bf")
+
+        def quantise_w1(half, o, c0, width, engine, grouped=None, codes=None):
+            name = "%d%d%d" % (half, o, c0)
+            if grouped is None:
+                grouped = tile([P, width, 4], BF16, "w1_bf" + name)[:]
+            dst = grouped.rearrange("p (c i) j -> p c j i", i=4)
+            src = w1_raw[half, o][:, :, c0 : c0 + width].rearrange("p j (c i) -> p c j i", i=4)
+            if engine == "vector":
+                nc.vector.tensor_copy(dst, src)
+            else:
+                nc.scalar.copy(dst, src)
+            if codes is None:
+                codes = tile([P, width], U32, "w1_codes" + name)
+            scales = tile([P, width], U8, "w1_scales" + name)
+            nc.vector.quantize_mx(codes[:].bitcast(FP8X4), scales[:], grouped.rearrange("p c j -> p (c j)"))
+            for b in range(width // P):
+                cols = slice(b * P, (b + 1) * P)
+                w1_q[half + c0 // P + b, o] = (codes[:, cols].bitcast(FP8X4), scales[:, cols])
+
+        f_neg = [tile([P, S], F32, "f_neg%d" % c) for c in range(4)]
+
+        def project(c, cols, engine, bank):
+            acc = banks[bank][:, 0 : cols.stop - cols.start]
+            for o in range(2):
+                codes, scales = w1_q[c, o]
+                nc.tensor.matmul_mx(acc, codes, scales, xw[o][:, cols].bitcast(FP8X4), xs[4 * o : P, cols], start=(o == 0), stop=(o == 1))
+            if engine == "vector":
+                nc.vector.tensor_scalar(f_neg[c][:, cols], acc, -1.0, None, MULT)
+            else:
+                nc.scalar.activation(f_neg[c][:, cols], acc, ACT.Copy, scale=-1.0)
+
+        terms = {}
+
+        def interpolate(c, h0, halves):
+            cols = slice(P * h0, P * (h0 + halves))
+            for d in range(2):
+                term = tile([P, P * halves], F32, "term%d%d%d" % (c, h0, d))
+                window = f_neg[c][:].indirect(pos_sb[d][:, 8 * h0 : 8 * (h0 + halves)])
+                nc.vector.tensor_tensor(term[:], window, gate_sb[:, d, cols], MULT)
+                for b in range(halves):
+                    terms[c, h0 + b, d] = term[:, P * b : P * (b + 1)]
+
+        z_t = [tile([P, H], BF16, "z_t%d" % h) for h in range(2)]
+
+        def difference(pair, h, bank):
+            e_t = banks[bank][:, 0 : 2 * P].rearrange("v (b i) -> v b i", b=2)
+            for b in range(2):
+                c = 2 * pair + b
+                parts = [terms[c, h, 0], ref_sb[:, c, P * h : P * (h + 1)], terms[c, h, 1]]
+                for n, part in enumerate(parts):
+                    nc.tensor.matmul(e_t[:, b, :], part, ident[:], start=(n == 0), stop=(n == 2), is_transpose=True)
+            dst = z_t[h][:].rearrange("v (u g q e) -> v g u q e", u=2, g=2, e=2)[:, pair]
+            src = e_t.rearrange("v b (q u e) -> v u (b q) e", u=2, e=2)
+            nc.scalar.activation(dst, src, ACT.Abs)
+
+        w2_codes = tile([P, N], U32, "w2_codes")
+        w2_scales = tile([P, N], U8, "w2_scales")
+
+        def quantise_w2():
+            grouped = last_bf
+            for g in range(4):
+                dst = grouped[:].rearrange("p (t m) j -> p m j t", t=4)[:, 32 * g : 32 * (g + 1)]
+                src = w2_raw[:].rearrange("p j (m t) -> p m j t", t=4)[:, 32 * g : 32 * (g + 1)]
+                nc.scalar.copy(dst, src)
+            nc.vector.quantize_mx(w2_codes[:].bitcast(FP8X4), w2_scales[:], grouped[:].rearrange("p c j -> p (c j)"))
+
+        y_scales = tile([P, V], U8, "y_scales")
+
+        def second_layer(h, bank_z, bank_y):
+            cols = slice(P * h, P * (h + 1))
+            words = z_t[h][:].bitcast(F32)
+            z_words = banks[bank_z][:, 0 : 2 * P].rearrange("p (u v) -> p u v", u=2)
+            for u in range(2):
+                nc.tensor.transpose(z_words[:, u, :], words[:, P * u : P * (u + 1)], ident[:])
+            z_bf = tile([P, P, 4], BF16, "z_bf%d" % h)
+            z_flat = z_bf[:].rearrange("p v t -> p (v t)")
+            nc.scalar.copy(z_flat.bitcast(F32).rearrange("p (v u) -> p v u", u=2), z_words.rearrange("p u v -> p v u"))
+            z_codes = tile([P, P], U32, "z_codes%d" % h)
+            z_scales = tile([P, P], U8, "z_scales%d" % h)
+            nc.vector.quantize_mx(z_codes[:].bitcast(FP8X4), z_scales[:], z_flat)
+            acc = banks[bank_y][:].rearrange("p (t v) -> p t v", t=4)
+            for t in range(4):
+                m = slice(P * t, P * (t + 1))
+                nc.tensor.matmul_mx(acc[:, t, :], w2_codes[:, m].bitcast(FP8X4), w2_scales[:, m], z_codes[:].bitcast(FP8X4), z_scales[:], start=True, stop=True)
+            y = tile([P, 4, P], F32, "y%d" % h)
+            nc.scalar.copy(y[:], acc)
+            nc.sync.dma_start(out_0.rearrange("(p t) v -> p t v", t=4)[:, :, cols], y[:])
+            y_bf = tile([P, P, 4], BF16, "y_bf%d" % h)
+            nc.vector.tensor_copy(y_bf[:].rearrange("p (c i) t -> p c t i", i=4), y[:].rearrange("p t (c i) -> p c t i", i=4))
+            y_codes = tile([P, P], U32, "y_codes%d" % h)
+            nc.vector.quantize_mx(y_codes[:].bitcast(FP8X4), y_scales[:, cols], y_bf[:].rearrange("p v t -> p (v t)"))
+            nc.sync.dma_start(out_1[0].rearrange("p c r -> p (c r)").bitcast(I32)[:, cols], y_codes[:].bitcast(I32))
+
+        quantise_w1(0, 0, 0, 128, "scalar")
+        pick_words(1, slice(0, 256))
+        quantise_w1(0, 1, 0, 128, "scalar", twice_bf[:], overlay.tile([P, P], U32, name="first_codes", offset=0, align_bytes=64))
+        pick_words(1, slice(256, 512))
+        project(0, slice(0, 256), "scalar", 0)
+        project(0, slice(256, 512), "vector", 1)
+        quantise_w1(1, 0, 0, 128, "scalar")
+        quantise_w1(1, 1, 0, 128, "vector", twice_bf[:])
+        project(1, slice(0, 512), "scalar", 2)
+        interpolate(0, 0, 2)
+        quantise_w1(2, 0, 0, 256, "scalar", overlay.tile([P, 256, 4], BF16, name="held_bf", offset=0, align_bytes=64)[:])
+        quantise_w1(2, 1, 0, 128, "scalar")
+        project(2, slice(0, 512), "scalar", 3)
+        interpolate(1, 0, 2)
+        quantise_w1(2, 1, 128, 128, "scalar", last_bf[:, 0:P, :])
+        project(3, slice(0, 512), "scalar", 4)
+        interpolate(2, 0, 1)
+        difference(0, 0, 3)
+        difference(0, 1, 4)
+        interpolate(3, 0, 1)
+        difference(1, 0, 0)
+        interpolate(2, 1, 1)
+        interpolate(3, 1, 1)
+        quantise_w2()
+        second_layer(0, 2, 6)
+        difference(1, 1, 1)
+        second_layer(1, 5, 7)
+        for q in range(4):
+            queue = nc.scalar if q % 2 else nc.sync
+            queue.dma_start(out_2[0, 4 * q : 4 * q + 4, :].bitcast(I32), y_scales[32 * q : 32 * q + 4, :].bitcast(I32))

@@ -32,17 +32,16 @@ def tile_picked_zwarp_abs_po_kernel(
         def tile(shape, dtype, name):
             return sb.tile(shape, dtype, name=name, align_bytes=64)
 
-        ident = tile([P, P], F32, "ident")
-        make_identity(nc, ident[:])
-
         offs_sb = lists.tile([P, S // 16], U16, name="offs_sb")
         pos_sb = [lists.tile([P, V // 16], U16, name="pos_sb%d" % d) for d in range(2)]
         nc.sync.dma_start(offs_sb[:], offs)
+        nc.sync.dma_start(pos_sb[0][:], pos1)
+        nc.sync.dma_start(pos_sb[1][:], pos2)
 
         xs_all = tile([P, T], U8, "xs_all")
         nc.vector.memset(xs_all[:].bitcast(I32), 0)
         for q in range(4):
-            nc.scalar.dma_start(xs_all[32 * q : 32 * q + 8, :].bitcast(I32), x_scales[:, 4 * q : 4 * q + 4, :].bitcast(I32))
+            nc.sync.dma_start(xs_all[32 * q : 32 * q + 8, :].bitcast(I32), x_scales[:, 4 * q : 4 * q + 4, :].bitcast(I32))
 
         xw_all = [tile([P, T], I32, "xw_all%d" % o) for o in range(2)]
         for o in range(2):
@@ -62,8 +61,6 @@ def tile_picked_zwarp_abs_po_kernel(
         nc.sync.dma_start(gate_sb[:], gate.rearrange("d p v -> p d v"))
         load_w1(1, 1, 0)
         load_w1(1, 1, 1)
-        nc.sync.dma_start(pos_sb[0][:], pos1)
-        nc.sync.dma_start(pos_sb[1][:], pos2)
         load_w1(2, 2, 0)
         load_w1(2, 2, 1)
         ref_sb = tile([P, 4, V], F32, "ref_sb")
@@ -71,6 +68,8 @@ def tile_picked_zwarp_abs_po_kernel(
         w2_raw = tile([P, 4, N], F32, "w2_raw")
         nc.sync.dma_start(w2_raw[:], w2.rearrange("(p j) m -> p j m", j=4))
 
+        ident = tile([P, P], F32, "ident")
+        make_identity(nc, ident[:])
         warm = tile([P, 1], F32, "warm")
         nc.scalar.activation(warm[:], ident[:, 0:1], ACT.Abs)
 
@@ -82,11 +81,13 @@ def tile_picked_zwarp_abs_po_kernel(
             nc.vector.tensor_copy(xw[o][:, cols], xw_all[o][:].bitcast(U32).indirect(offsets))
 
         pick_words(0, slice(0, S))
+        pick_words(1, slice(0, 256))
         nc.vector.tensor_copy(xs[:], xs_all[:].indirect(offs_sb[:]))
 
         w1_q = {}
-        twice_bf = tile([P, P, 4], BF16, "twice_bf")
-        last_bf = tile([P, N, 4], BF16, "last_bf")
+
+        def shared(shape, dtype, name, offset):
+            return overlay.tile(shape, dtype, name=name, offset=offset, align_bytes=64)
 
         def quantise_w1(half, o, c0, width, engine, grouped=None, codes=None):
             name = "%d%d%d" % (half, o, c0)
@@ -120,10 +121,14 @@ def tile_picked_zwarp_abs_po_kernel(
 
         terms = {}
 
-        def interpolate(c, h0, halves):
+        def interpolate(c, h0, halves, offsets=None):
             cols = slice(P * h0, P * (h0 + halves))
             for d in range(2):
-                term = tile([P, P * halves], F32, "term%d%d%d" % (c, h0, d))
+                name = "term%d%d%d" % (c, h0, d)
+                if offsets is None:
+                    term = tile([P, P * halves], F32, name)
+                else:
+                    term = shared([P, P * halves], F32, name, offsets[d])
                 window = f_neg[c][:].indirect(pos_sb[d][:, 8 * h0 : 8 * (h0 + halves)])
                 nc.vector.tensor_tensor(term[:], window, gate_sb[:, d, cols], MULT)
                 for b in range(halves):
@@ -131,14 +136,14 @@ def tile_picked_zwarp_abs_po_kernel(
 
         z_t = [tile([P, H], BF16, "z_t%d" % h) for h in range(2)]
 
-        def difference(pair, h, bank):
-            e_t = banks[bank][:, 0 : 2 * P].rearrange("v (b i) -> v b i", b=2)
-            for b in range(2):
-                c = 2 * pair + b
+        def difference(c0, chunks, h, bank):
+            e_t = banks[bank][:, 0 : chunks * P].rearrange("v (b i) -> v b i", b=chunks)
+            for b in range(chunks):
+                c = c0 + b
                 parts = [terms[c, h, 0], ref_sb[:, c, P * h : P * (h + 1)], terms[c, h, 1]]
                 for n, part in enumerate(parts):
                     nc.tensor.matmul(e_t[:, b, :], part, ident[:], start=(n == 0), stop=(n == 2), is_transpose=True)
-            dst = z_t[h][:].rearrange("v (u g q e) -> v g u q e", u=2, g=2, e=2)[:, pair]
+            dst = z_t[h][:].rearrange("v (u q e) -> v u q e", u=2, e=2)[:, :, 32 * c0 : 32 * (c0 + chunks), :]
             src = e_t.rearrange("v b (q u e) -> v u (b q) e", u=2, e=2)
             nc.scalar.activation(dst, src, ACT.Abs)
 
@@ -146,27 +151,33 @@ def tile_picked_zwarp_abs_po_kernel(
         w2_scales = tile([P, N], U8, "w2_scales")
 
         def quantise_w2():
-            grouped = last_bf
+            grouped = shared([P, N, 4], BF16, "w2_bf", 2048)
             for g in range(4):
                 dst = grouped[:].rearrange("p (t m) j -> p m j t", t=4)[:, 32 * g : 32 * (g + 1)]
                 src = w2_raw[:].rearrange("p j (m t) -> p m j t", t=4)[:, 32 * g : 32 * (g + 1)]
                 nc.scalar.copy(dst, src)
             nc.vector.quantize_mx(w2_codes[:].bitcast(FP8X4), w2_scales[:], grouped[:].rearrange("p c j -> p (c j)"))
 
+        z_q = {}
         y_scales = tile([P, V], U8, "y_scales")
 
-        def second_layer(h, bank_z, bank_y):
-            cols = slice(P * h, P * (h + 1))
+        def quantise_z(h, bank_z):
             words = z_t[h][:].bitcast(F32)
             z_words = banks[bank_z][:, 0 : 2 * P].rearrange("p (u v) -> p u v", u=2)
             for u in range(2):
                 nc.tensor.transpose(z_words[:, u, :], words[:, P * u : P * (u + 1)], ident[:])
             z_bf = tile([P, P, 4], BF16, "z_bf%d" % h)
             z_flat = z_bf[:].rearrange("p v t -> p (v t)")
-            nc.scalar.copy(z_flat.bitcast(F32).rearrange("p (v u) -> p v u", u=2), z_words.rearrange("p u v -> p v u"))
+            copy = nc.scalar.copy if h else nc.vector.tensor_copy
+            copy(z_flat.bitcast(F32).rearrange("p (v u) -> p v u", u=2), z_words.rearrange("p u v -> p v u"))
             z_codes = tile([P, P], U32, "z_codes%d" % h)
             z_scales = tile([P, P], U8, "z_scales%d" % h)
             nc.vector.quantize_mx(z_codes[:].bitcast(FP8X4), z_scales[:], z_flat)
+            z_q[h] = (z_codes, z_scales)
+
+        def second_layer(h, bank_y):
+            cols = slice(P * h, P * (h + 1))
+            z_codes, z_scales = z_q[h]
             acc = banks[bank_y][:].rearrange("p (t v) -> p t v", t=4)
             for t in range(4):
                 m = slice(P * t, P * (t + 1))
@@ -181,32 +192,34 @@ def tile_picked_zwarp_abs_po_kernel(
             nc.sync.dma_start(out_1[0].rearrange("p c r -> p (c r)").bitcast(I32)[:, cols], y_codes[:].bitcast(I32))
 
         quantise_w1(0, 0, 0, 128, "scalar")
-        pick_words(1, slice(0, 256))
-        quantise_w1(0, 1, 0, 128, "scalar", twice_bf[:], overlay.tile([P, P], U32, name="first_codes", offset=0, align_bytes=64))
+        quantise_w1(0, 1, 0, 128, "scalar")
         pick_words(1, slice(256, 512))
-        project(0, slice(0, 256), "scalar", 0)
+        project(0, slice(0, 256), "vector", 0)
         project(0, slice(256, 512), "vector", 1)
         quantise_w1(1, 0, 0, 128, "scalar")
-        quantise_w1(1, 1, 0, 128, "vector", twice_bf[:])
-        project(1, slice(0, 512), "scalar", 2)
+        quantise_w1(1, 1, 0, 128, "scalar", codes=shared([P, P], U32, "codes11", 1024))
         interpolate(0, 0, 2)
-        quantise_w1(2, 0, 0, 256, "scalar", overlay.tile([P, 256, 4], BF16, name="held_bf", offset=0, align_bytes=64)[:])
-        quantise_w1(2, 1, 0, 128, "scalar")
+        quantise_w1(2, 0, 0, 256, "scalar")
+        quantise_w1(2, 1, 0, 128, "scalar", shared([P, P, 4], BF16, "grouped21", 0)[:])
+        project(1, slice(0, 512), "scalar", 2)
+        quantise_w1(2, 1, 128, 128, "scalar", shared([P, P, 4], BF16, "grouped31", 1024)[:], shared([P, P], U32, "codes31", 2048))
+        interpolate(1, 0, 2, (0, 1024))
         project(2, slice(0, 512), "scalar", 3)
-        interpolate(1, 0, 2)
-        quantise_w1(2, 1, 128, 128, "scalar", last_bf[:, 0:P, :])
         project(3, slice(0, 512), "scalar", 4)
         interpolate(2, 0, 1)
-        difference(0, 0, 3)
-        difference(0, 1, 4)
+        difference(0, 2, 0, 3)
+        difference(0, 2, 1, 4)
         interpolate(3, 0, 1)
-        difference(1, 0, 0)
+        difference(2, 2, 0, 0)
         interpolate(2, 1, 1)
+        difference(2, 1, 1, 1)
         interpolate(3, 1, 1)
         quantise_w2()
-        second_layer(0, 2, 6)
-        difference(1, 1, 1)
-        second_layer(1, 5, 7)
+        quantise_z(0, 5)
+        difference(3, 1, 1, 2)
+        quantise_z(1, 0)
+        second_layer(0, 6)
+        second_layer(1, 7)
         for q in range(4):
             queue = nc.scalar if q % 2 else nc.sync
             queue.dma_start(out_2[0, 4 * q : 4 * q + 4, :].bitcast(I32), y_scales[32 * q : 32 * q + 4, :].bitcast(I32))

@@ -36,16 +36,22 @@ def tile_picked_zwarp_abs_po_kernel(
         pos_sb = [lists.tile([P, V // 16], U16, name="pos_sb%d" % d) for d in range(2)]
         nc.sync.dma_start(offs_sb[:], offs)
         nc.sync.dma_start(pos_sb[0][:], pos1)
-        nc.sync.dma_start(pos_sb[1][:], pos2)
+
+        xw_all = [tile([P, T], I32, "xw_all%d" % o) for o in range(2)]
+
+        def load_words(o):
+            nc.sync.dma_start(xw_all[o][:], x_words[o].rearrange("p c r -> p (c r)").bitcast(I32))
+
+        load_words(0)
+        gate_rows = tile([P, P], F32, "gate_rows")
+        nc.gpsimd.memset(gate_rows[:], 0.0)
+        nc.sync.dma_start(gate_rows[0:4, :], gate[:, 0, :].rearrange("d (h k) -> d h k", h=2))
 
         xs_all = tile([P, T], U8, "xs_all")
         nc.vector.memset(xs_all[:].bitcast(I32), 0)
         for q in range(4):
             nc.sync.dma_start(xs_all[32 * q : 32 * q + 8, :].bitcast(I32), x_scales[:, 4 * q : 4 * q + 4, :].bitcast(I32))
-
-        xw_all = [tile([P, T], I32, "xw_all%d" % o) for o in range(2)]
-        for o in range(2):
-            nc.sync.dma_start(xw_all[o][:], x_words[o].rearrange("p c r -> p (c r)").bitcast(I32))
+        load_words(1)
 
         w1_raw = {}
 
@@ -57,8 +63,7 @@ def tile_picked_zwarp_abs_po_kernel(
 
         load_w1(0, 1, 0)
         load_w1(0, 1, 1)
-        gate_sb = tile([P, 2, V], F32, "gate_sb")
-        nc.sync.dma_start(gate_sb[:], gate.rearrange("d p v -> p d v"))
+        nc.sync.dma_start(pos_sb[1][:], pos2)
         load_w1(1, 1, 0)
         load_w1(1, 1, 1)
         load_w1(2, 2, 0)
@@ -73,6 +78,13 @@ def tile_picked_zwarp_abs_po_kernel(
         warm = tile([P, 1], F32, "warm")
         nc.scalar.activation(warm[:], ident[:, 0:1], ACT.Abs)
 
+        nc.tensor.transpose(banks[5][:, 0:P], gate_rows[:], ident[:])
+        gate_cols = tile([P, 4], F32, "gate_cols")
+        nc.scalar.activation(gate_cols[:], banks[5][:, 0:4], ACT.Copy, scale=-1.0)
+        for n in range(4):
+            nc.tensor.transpose(banks[6][:, P * n : P * (n + 1)], gate_cols[:, n : n + 1].to_broadcast([P, P]), ident[:])
+        gate_sb = tile([P, 2, V], F32, "gate_sb")
+
         xs = tile([P, S], U8, "xs")
         xw = [tile([P, S], U32, "xw%d" % o) for o in range(2)]
 
@@ -81,8 +93,8 @@ def tile_picked_zwarp_abs_po_kernel(
             nc.vector.tensor_copy(xw[o][:, cols], xw_all[o][:].bitcast(U32).indirect(offsets))
 
         pick_words(0, slice(0, S))
-        pick_words(1, slice(0, 256))
         nc.vector.tensor_copy(xs[:], xs_all[:].indirect(offs_sb[:]))
+        pick_words(1, slice(0, 256))
 
         w1_q = {}
 
@@ -115,9 +127,9 @@ def tile_picked_zwarp_abs_po_kernel(
                 codes, scales = w1_q[c, o]
                 nc.tensor.matmul_mx(acc, codes, scales, xw[o][:, cols].bitcast(FP8X4), xs[4 * o : P, cols], start=(o == 0), stop=(o == 1))
             if engine == "vector":
-                nc.vector.tensor_scalar(f_neg[c][:, cols], acc, -1.0, None, MULT)
+                nc.vector.tensor_copy(f_neg[c][:, cols], acc)
             else:
-                nc.scalar.activation(f_neg[c][:, cols], acc, ACT.Copy, scale=-1.0)
+                nc.scalar.copy(f_neg[c][:, cols], acc)
 
         terms = {}
 
@@ -175,29 +187,55 @@ def tile_picked_zwarp_abs_po_kernel(
             nc.vector.quantize_mx(z_codes[:].bitcast(FP8X4), z_scales[:], z_flat)
             z_q[h] = (z_codes, z_scales)
 
-        def second_layer(h, bank_y):
-            cols = slice(P * h, P * (h + 1))
+        out_rows = out_0.rearrange("(p t) v -> p t v", t=4)
+
+        def product(h, t, acc):
             z_codes, z_scales = z_q[h]
-            acc = banks[bank_y][:].rearrange("p (t v) -> p t v", t=4)
-            for t in range(4):
-                m = slice(P * t, P * (t + 1))
-                nc.tensor.matmul_mx(acc[:, t, :], w2_codes[:, m].bitcast(FP8X4), w2_scales[:, m], z_codes[:].bitcast(FP8X4), z_scales[:], start=True, stop=True)
-            y = tile([P, 4, P], F32, "y%d" % h)
-            nc.scalar.copy(y[:], acc)
-            nc.sync.dma_start(out_0.rearrange("(p t) v -> p t v", t=4)[:, :, cols], y[:])
-            y_bf = tile([P, P, 4], BF16, "y_bf%d" % h)
-            nc.vector.tensor_copy(y_bf[:].rearrange("p (c i) t -> p c t i", i=4), y[:].rearrange("p t (c i) -> p c t i", i=4))
+            m = slice(P * t, P * (t + 1))
+            nc.tensor.matmul_mx(acc, w2_codes[:, m].bitcast(FP8X4), w2_scales[:, m], z_codes[:].bitcast(FP8X4), z_scales[:], start=True, stop=True)
+
+        def store_planes(h, y_bf):
+            cols = slice(P * h, P * (h + 1))
             y_codes = tile([P, P], U32, "y_codes%d" % h)
             nc.vector.quantize_mx(y_codes[:].bitcast(FP8X4), y_scales[:, cols], y_bf[:].rearrange("p v t -> p (v t)"))
             nc.sync.dma_start(out_1[0].rearrange("p c r -> p (c r)").bitcast(I32)[:, cols], y_codes[:].bitcast(I32))
 
+        def second_layer(h, bank_y):
+            cols = slice(P * h, P * (h + 1))
+            acc = banks[bank_y][:].rearrange("p (t v) -> p t v", t=4)
+            for t in range(4):
+                product(h, t, acc[:, t, :])
+            y = tile([P, 4, P], F32, "y%d" % h)
+            nc.scalar.copy(y[:], acc)
+            nc.sync.dma_start(out_rows[:, :, cols], y[:])
+            y_bf = tile([P, P, 4], BF16, "y_bf%d" % h)
+            nc.vector.tensor_copy(y_bf[:].rearrange("p (c i) t -> p c t i", i=4), y[:].rearrange("p t (c i) -> p c t i", i=4))
+            store_planes(h, y_bf)
+
+        def second_layer_split(h, bank_low, bank_high):
+            cols = slice(P * h, P * (h + 1))
+            low = banks[bank_low][:, 0 : 2 * P].rearrange("p (t v) -> p t v", t=2)
+            high = banks[bank_high][:, 0 : 2 * P].rearrange("p (t v) -> p t v", t=2)
+            for t in range(4):
+                product(h, t, (low, high)[t // 2][:, t % 2, :])
+            y = tile([P, 4, P], F32, "y%d" % h)
+            y_bf = tile([P, P, 4], BF16, "y_bf%d" % h)
+            nc.vector.tensor_copy(y_bf[:, :, 0:2], low.rearrange("p t v -> p v t"))
+            nc.scalar.copy(y[:, 2:4, :], high)
+            nc.scalar.copy(y[:, 0:2, :], low)
+            nc.sync.dma_start(out_rows[:, :, cols], y[:])
+            nc.vector.tensor_copy(y_bf[:, :, 2:4], y[:, 2:4, :].rearrange("p t v -> p v t"))
+            store_planes(h, y_bf)
+
         quantise_w1(0, 0, 0, 128, "scalar")
-        quantise_w1(0, 1, 0, 128, "scalar")
         pick_words(1, slice(256, 512))
+        quantise_w1(0, 1, 0, 128, "scalar")
         project(0, slice(0, 256), "vector", 0)
         project(0, slice(256, 512), "vector", 1)
         quantise_w1(1, 0, 0, 128, "scalar")
         quantise_w1(1, 1, 0, 128, "scalar", codes=shared([P, P], U32, "codes11", 1024))
+        for d in range(2):
+            nc.scalar.copy(gate_sb[:, d, :], banks[6][:, V * d : V * (d + 1)])
         interpolate(0, 0, 2)
         quantise_w1(2, 0, 0, 256, "scalar")
         quantise_w1(2, 1, 0, 128, "scalar", shared([P, P, 4], BF16, "grouped21", 0)[:])
@@ -219,7 +257,7 @@ def tile_picked_zwarp_abs_po_kernel(
         difference(3, 1, 1, 2)
         quantise_z(1, 0)
         second_layer(0, 6)
-        second_layer(1, 7)
+        second_layer_split(1, 7, 3)
         for q in range(4):
             queue = nc.scalar if q % 2 else nc.sync
             queue.dma_start(out_2[0, 4 * q : 4 * q + 4, :].bitcast(I32), y_scales[32 * q : 32 * q + 4, :].bitcast(I32))

@@ -15,7 +15,13 @@ ACT = mybir.ActivationFunctionType
 
 P = 128
 K, T, S, V, H, N = 1024, 1024, 512, 256, 512, 512
+PASS = 512
 FLOPS = 2 * K * H * S + 2 * H * N * V
+
+CHUNK2_REGION = 0
+CHUNK3_REGION = 1024
+W2_REGION = 2048
+W2_PIECES = 4
 
 
 def tile_picked_zwarp_abs_po_kernel(
@@ -29,8 +35,10 @@ def tile_picked_zwarp_abs_po_kernel(
         psum = ctx.enter_context(tc.psum_pool(name="psum", bufs=1))
         banks = [psum.tile([P, 512], F32, name="bank%d" % b) for b in range(8)]
 
-        def tile(shape, dtype, name):
-            return sb.tile(shape, dtype, name=name, align_bytes=64)
+        def tile(shape, dtype, name, region=None):
+            if region is None:
+                return sb.tile(shape, dtype, name=name, align_bytes=64)
+            return overlay.tile(shape, dtype, name=name, offset=region, align_bytes=64)
 
         offs_sb = lists.tile([P, S // 16], U16, name="offs_sb")
         pos_sb = [lists.tile([P, V // 16], U16, name="pos_sb%d" % d) for d in range(2)]
@@ -43,24 +51,26 @@ def tile_picked_zwarp_abs_po_kernel(
             nc.sync.dma_start(xw_all[o][:], x_words[o].rearrange("p c r -> p (c r)").bitcast(I32))
 
         load_words(0)
+
         gate_rows = tile([P, P], F32, "gate_rows")
         nc.gpsimd.memset(gate_rows[:], 0.0)
-        nc.sync.dma_start(gate_rows[0:4, :], gate[:, 0, :].rearrange("d (h k) -> d h k", h=2))
+        nc.sync.dma_start(gate_rows[0:4, :], gate[:, 0, :].rearrange("d (h v) -> d h v", h=2))
 
         xs_all = tile([P, T], U8, "xs_all")
         nc.vector.memset(xs_all[:].bitcast(I32), 0)
         for q in range(4):
             nc.sync.dma_start(xs_all[32 * q : 32 * q + 8, :].bitcast(I32), x_scales[:, 4 * q : 4 * q + 4, :].bitcast(I32))
-        load_words(1)
 
         w1_raw = {}
 
-        def load_w1(c, chunks, o):
-            raw = tile([P, 4, P * chunks], F32, "w1_raw%d%d" % (c, o))
-            rows = w1[512 * o : 512 * (o + 1), P * c : P * (c + chunks)]
+        def load_w1(c0, chunks, o):
+            raw = tile([P, 4, P * chunks], F32, "w1_raw%d%d" % (c0, o))
+            rows = w1[PASS * o : PASS * (o + 1), P * c0 : P * (c0 + chunks)]
             nc.sync.dma_start(raw[:], rows.rearrange("(p j) c -> p j c", j=4))
-            w1_raw[c, o] = raw
+            for b in range(chunks):
+                w1_raw[c0 + b, o] = (raw, P * b)
 
+        load_words(1)
         load_w1(0, 1, 0)
         load_w1(0, 1, 1)
         nc.sync.dma_start(pos_sb[1][:], pos2)
@@ -75,15 +85,13 @@ def tile_picked_zwarp_abs_po_kernel(
 
         ident = tile([P, P], F32, "ident")
         make_identity(nc, ident[:])
-        warm = tile([P, 1], F32, "warm")
-        nc.scalar.activation(warm[:], ident[:, 0:1], ACT.Abs)
 
         nc.tensor.transpose(banks[5][:, 0:P], gate_rows[:], ident[:])
         gate_cols = tile([P, 4], F32, "gate_cols")
         nc.scalar.activation(gate_cols[:], banks[5][:, 0:4], ACT.Copy, scale=-1.0)
         for n in range(4):
             nc.tensor.transpose(banks[6][:, P * n : P * (n + 1)], gate_cols[:, n : n + 1].to_broadcast([P, P]), ident[:])
-        gate_sb = tile([P, 2, V], F32, "gate_sb")
+        neg_gate = tile([P, 2, V], F32, "neg_gate")
 
         xs = tile([P, S], U8, "xs")
         xw = [tile([P, S], U32, "xw%d" % o) for o in range(2)]
@@ -92,57 +100,40 @@ def tile_picked_zwarp_abs_po_kernel(
             offsets = offs_sb[:, cols.start // 16 : cols.stop // 16]
             nc.vector.tensor_copy(xw[o][:, cols], xw_all[o][:].bitcast(U32).indirect(offsets))
 
-        pick_words(0, slice(0, S))
-        nc.vector.tensor_copy(xs[:], xs_all[:].indirect(offs_sb[:]))
-        pick_words(1, slice(0, 256))
-
         w1_q = {}
 
-        def shared(shape, dtype, name, offset):
-            return overlay.tile(shape, dtype, name=name, offset=offset, align_bytes=64)
-
-        def quantise_w1(half, o, c0, width, engine, grouped=None, codes=None):
-            name = "%d%d%d" % (half, o, c0)
-            if grouped is None:
-                grouped = tile([P, width, 4], BF16, "w1_bf" + name)[:]
-            dst = grouped.rearrange("p (c i) j -> p c j i", i=4)
-            src = w1_raw[half, o][:, :, c0 : c0 + width].rearrange("p j (c i) -> p c j i", i=4)
-            if engine == "vector":
-                nc.vector.tensor_copy(dst, src)
-            else:
-                nc.scalar.copy(dst, src)
-            if codes is None:
-                codes = tile([P, width], U32, "w1_codes" + name)
-            scales = tile([P, width], U8, "w1_scales" + name)
-            nc.vector.quantize_mx(codes[:].bitcast(FP8X4), scales[:], grouped.rearrange("p c j -> p (c j)"))
-            for b in range(width // P):
+        def quantise_w1(c0, chunks, o, bf_region=None, codes_region=None):
+            raw, first = w1_raw[c0, o]
+            width = P * chunks
+            grouped = tile([P, width, 4], BF16, "w1_bf%d%d" % (c0, o), bf_region)
+            nc.scalar.copy(
+                grouped[:].rearrange("p (c n) j -> p c j n", n=4),
+                raw[:, :, first : first + width].rearrange("p j (c n) -> p c j n", n=4),
+            )
+            codes = tile([P, width], U32, "w1_codes%d%d" % (c0, o), codes_region)
+            scales = tile([P, width], U8, "w1_scales%d%d" % (c0, o))
+            nc.vector.quantize_mx(codes[:].bitcast(FP8X4), scales[:], grouped[:].rearrange("p c j -> p (c j)"))
+            for b in range(chunks):
                 cols = slice(b * P, (b + 1) * P)
-                w1_q[half + c0 // P + b, o] = (codes[:, cols].bitcast(FP8X4), scales[:, cols])
+                w1_q[c0 + b, o] = (codes[:, cols].bitcast(FP8X4), scales[:, cols])
 
-        f_neg = [tile([P, S], F32, "f_neg%d" % c) for c in range(4)]
+        f = [tile([P, S], F32, "f%d" % c) for c in range(4)]
 
-        def project(c, cols, engine, bank):
+        def project(c, cols, copy, bank):
             acc = banks[bank][:, 0 : cols.stop - cols.start]
             for o in range(2):
                 codes, scales = w1_q[c, o]
                 nc.tensor.matmul_mx(acc, codes, scales, xw[o][:, cols].bitcast(FP8X4), xs[4 * o : P, cols], start=(o == 0), stop=(o == 1))
-            if engine == "vector":
-                nc.vector.tensor_copy(f_neg[c][:, cols], acc)
-            else:
-                nc.scalar.copy(f_neg[c][:, cols], acc)
+            copy(f[c][:, cols], acc)
 
         terms = {}
 
-        def interpolate(c, h0, halves, offsets=None):
+        def interpolate(c, h0, halves, regions=(None, None)):
             cols = slice(P * h0, P * (h0 + halves))
             for d in range(2):
-                name = "term%d%d%d" % (c, h0, d)
-                if offsets is None:
-                    term = tile([P, P * halves], F32, name)
-                else:
-                    term = shared([P, P * halves], F32, name, offsets[d])
-                window = f_neg[c][:].indirect(pos_sb[d][:, 8 * h0 : 8 * (h0 + halves)])
-                nc.vector.tensor_tensor(term[:], window, gate_sb[:, d, cols], MULT)
+                term = tile([P, P * halves], F32, "term%d%d%d" % (c, h0, d), regions[d])
+                window = f[c][:].indirect(pos_sb[d][:, cols.start // 16 : cols.stop // 16])
+                nc.vector.tensor_tensor(term[:], window, neg_gate[:, d, cols], MULT)
                 for b in range(halves):
                     terms[c, h0 + b, d] = term[:, P * b : P * (b + 1)]
 
@@ -155,95 +146,100 @@ def tile_picked_zwarp_abs_po_kernel(
                 parts = [terms[c, h, 0], ref_sb[:, c, P * h : P * (h + 1)], terms[c, h, 1]]
                 for n, part in enumerate(parts):
                     nc.tensor.matmul(e_t[:, b, :], part, ident[:], start=(n == 0), stop=(n == 2), is_transpose=True)
-            dst = z_t[h][:].rearrange("v (u q e) -> v u q e", u=2, e=2)[:, :, 32 * c0 : 32 * (c0 + chunks), :]
-            src = e_t.rearrange("v b (q u e) -> v u (b q) e", u=2, e=2)
-            nc.scalar.activation(dst, src, ACT.Abs)
+            nc.scalar.activation(
+                z_t[h][:].rearrange("v (u p e) -> v u p e", u=2, e=2)[:, :, 32 * c0 : 32 * (c0 + chunks), :],
+                e_t.rearrange("v b (q u e) -> v u (b q) e", u=2, e=2),
+                ACT.Abs,
+            )
+
+        z_q = {}
+
+        def quantise_z(h, copy, bank):
+            words = z_t[h][:].bitcast(F32)
+            z_words = banks[bank][:, 0 : 2 * P].rearrange("p (u v) -> p u v", u=2)
+            for u in range(2):
+                nc.tensor.transpose(z_words[:, u, :], words[:, P * u : P * (u + 1)], ident[:])
+            z_bf = tile([P, 4 * P], BF16, "z_bf%d" % h)
+            copy(z_bf[:].bitcast(F32).rearrange("p (v u) -> p v u", u=2), z_words.rearrange("p u v -> p v u"))
+            z_codes = tile([P, P], U32, "z_codes%d" % h)
+            z_scales = tile([P, P], U8, "z_scales%d" % h)
+            nc.vector.quantize_mx(z_codes[:].bitcast(FP8X4), z_scales[:], z_bf[:])
+            z_q[h] = (z_codes, z_scales)
 
         w2_codes = tile([P, N], U32, "w2_codes")
         w2_scales = tile([P, N], U8, "w2_scales")
 
         def quantise_w2():
-            grouped = shared([P, N, 4], BF16, "w2_bf", 2048)
-            for g in range(4):
-                dst = grouped[:].rearrange("p (t m) j -> p m j t", t=4)[:, 32 * g : 32 * (g + 1)]
-                src = w2_raw[:].rearrange("p j (m t) -> p m j t", t=4)[:, 32 * g : 32 * (g + 1)]
-                nc.scalar.copy(dst, src)
+            grouped = tile([P, N, 4], BF16, "w2_bf", W2_REGION)
+            piece = P // W2_PIECES
+            for g in range(W2_PIECES):
+                nc.scalar.copy(
+                    grouped[:].rearrange("p (t r) j -> p r j t", t=4)[:, piece * g : piece * (g + 1)],
+                    w2_raw[:].rearrange("p j (r t) -> p r j t", t=4)[:, piece * g : piece * (g + 1)],
+                )
             nc.vector.quantize_mx(w2_codes[:].bitcast(FP8X4), w2_scales[:], grouped[:].rearrange("p c j -> p (c j)"))
 
-        z_q = {}
+        out_rows = out_0.rearrange("(r t) v -> r t v", t=4)
+        out_words = out_1[0].rearrange("r c t -> r (c t)").bitcast(I32)
         y_scales = tile([P, V], U8, "y_scales")
 
-        def quantise_z(h, bank_z):
-            words = z_t[h][:].bitcast(F32)
-            z_words = banks[bank_z][:, 0 : 2 * P].rearrange("p (u v) -> p u v", u=2)
-            for u in range(2):
-                nc.tensor.transpose(z_words[:, u, :], words[:, P * u : P * (u + 1)], ident[:])
-            z_bf = tile([P, P, 4], BF16, "z_bf%d" % h)
-            z_flat = z_bf[:].rearrange("p v t -> p (v t)")
-            copy = nc.scalar.copy if h else nc.vector.tensor_copy
-            copy(z_flat.bitcast(F32).rearrange("p (v u) -> p v u", u=2), z_words.rearrange("p u v -> p v u"))
-            z_codes = tile([P, P], U32, "z_codes%d" % h)
-            z_scales = tile([P, P], U8, "z_scales%d" % h)
-            nc.vector.quantize_mx(z_codes[:].bitcast(FP8X4), z_scales[:], z_flat)
-            z_q[h] = (z_codes, z_scales)
-
-        out_rows = out_0.rearrange("(p t) v -> p t v", t=4)
-
-        def product(h, t, acc):
+        def multiply_w2(h, t, acc):
             z_codes, z_scales = z_q[h]
             m = slice(P * t, P * (t + 1))
             nc.tensor.matmul_mx(acc, w2_codes[:, m].bitcast(FP8X4), w2_scales[:, m], z_codes[:].bitcast(FP8X4), z_scales[:], start=True, stop=True)
 
-        def store_planes(h, y_bf):
+        def quantise_y(h, y_bf):
             cols = slice(P * h, P * (h + 1))
             y_codes = tile([P, P], U32, "y_codes%d" % h)
-            nc.vector.quantize_mx(y_codes[:].bitcast(FP8X4), y_scales[:, cols], y_bf[:].rearrange("p v t -> p (v t)"))
-            nc.sync.dma_start(out_1[0].rearrange("p c r -> p (c r)").bitcast(I32)[:, cols], y_codes[:].bitcast(I32))
+            nc.vector.quantize_mx(y_codes[:].bitcast(FP8X4), y_scales[:, cols], y_bf[:].rearrange("r v t -> r (v t)"))
+            nc.sync.dma_start(out_words[:, cols], y_codes[:].bitcast(I32))
 
-        def second_layer(h, bank_y):
-            cols = slice(P * h, P * (h + 1))
-            acc = banks[bank_y][:].rearrange("p (t v) -> p t v", t=4)
+        def output_one_bank(h, bank):
+            acc = banks[bank][:].rearrange("r (t v) -> r t v", t=4)
             for t in range(4):
-                product(h, t, acc[:, t, :])
+                multiply_w2(h, t, acc[:, t, :])
             y = tile([P, 4, P], F32, "y%d" % h)
             nc.scalar.copy(y[:], acc)
-            nc.sync.dma_start(out_rows[:, :, cols], y[:])
+            nc.sync.dma_start(out_rows[:, :, P * h : P * (h + 1)], y[:])
             y_bf = tile([P, P, 4], BF16, "y_bf%d" % h)
-            nc.vector.tensor_copy(y_bf[:].rearrange("p (c i) t -> p c t i", i=4), y[:].rearrange("p t (c i) -> p c t i", i=4))
-            store_planes(h, y_bf)
+            nc.vector.tensor_copy(y_bf[:].rearrange("r (c n) t -> r c t n", n=4), y[:].rearrange("r t (c n) -> r c t n", n=4))
+            quantise_y(h, y_bf)
 
-        def second_layer_split(h, bank_low, bank_high):
-            cols = slice(P * h, P * (h + 1))
-            low = banks[bank_low][:, 0 : 2 * P].rearrange("p (t v) -> p t v", t=2)
-            high = banks[bank_high][:, 0 : 2 * P].rearrange("p (t v) -> p t v", t=2)
+        def output_two_banks(h, bank_low, bank_high):
+            low = banks[bank_low][:, 0 : 2 * P].rearrange("r (t v) -> r t v", t=2)
+            high = banks[bank_high][:, 0 : 2 * P].rearrange("r (t v) -> r t v", t=2)
             for t in range(4):
-                product(h, t, (low, high)[t // 2][:, t % 2, :])
+                multiply_w2(h, t, (low, high)[t // 2][:, t % 2, :])
             y = tile([P, 4, P], F32, "y%d" % h)
             y_bf = tile([P, P, 4], BF16, "y_bf%d" % h)
-            nc.vector.tensor_copy(y_bf[:, :, 0:2], low.rearrange("p t v -> p v t"))
+            nc.vector.tensor_copy(y_bf[:, :, 0:2], low.rearrange("r t v -> r v t"))
             nc.scalar.copy(y[:, 2:4, :], high)
             nc.scalar.copy(y[:, 0:2, :], low)
-            nc.sync.dma_start(out_rows[:, :, cols], y[:])
-            nc.vector.tensor_copy(y_bf[:, :, 2:4], y[:, 2:4, :].rearrange("p t v -> p v t"))
-            store_planes(h, y_bf)
+            nc.sync.dma_start(out_rows[:, :, P * h : P * (h + 1)], y[:])
+            nc.vector.tensor_copy(y_bf[:, :, 2:4], y[:, 2:4, :].rearrange("r t v -> r v t"))
+            quantise_y(h, y_bf)
 
-        quantise_w1(0, 0, 0, 128, "scalar")
-        pick_words(1, slice(256, 512))
-        quantise_w1(0, 1, 0, 128, "scalar")
-        project(0, slice(0, 256), "vector", 0)
-        project(0, slice(256, 512), "vector", 1)
-        quantise_w1(1, 0, 0, 128, "scalar")
-        quantise_w1(1, 1, 0, 128, "scalar", codes=shared([P, P], U32, "codes11", 1024))
+        left, right, whole = slice(0, S // 2), slice(S // 2, S), slice(0, S)
+        pick_words(0, whole)
+        nc.vector.tensor_copy(xs[:], xs_all[:].indirect(offs_sb[:]))
+        pick_words(1, left)
+        quantise_w1(0, 1, 0)
+        pick_words(1, right)
+        quantise_w1(0, 1, 1)
+        project(0, left, nc.vector.tensor_copy, 0)
+        project(0, right, nc.vector.tensor_copy, 1)
+        quantise_w1(1, 1, 0)
+        quantise_w1(1, 1, 1, codes_region=CHUNK3_REGION)
         for d in range(2):
-            nc.scalar.copy(gate_sb[:, d, :], banks[6][:, V * d : V * (d + 1)])
+            nc.scalar.copy(neg_gate[:, d, :], banks[6][:, V * d : V * (d + 1)])
         interpolate(0, 0, 2)
-        quantise_w1(2, 0, 0, 256, "scalar")
-        quantise_w1(2, 1, 0, 128, "scalar", shared([P, P, 4], BF16, "grouped21", 0)[:])
-        project(1, slice(0, 512), "scalar", 2)
-        quantise_w1(2, 1, 128, 128, "scalar", shared([P, P, 4], BF16, "grouped31", 1024)[:], shared([P, P], U32, "codes31", 2048))
-        interpolate(1, 0, 2, (0, 1024))
-        project(2, slice(0, 512), "scalar", 3)
-        project(3, slice(0, 512), "scalar", 4)
+        quantise_w1(2, 2, 0)
+        quantise_w1(2, 1, 1, bf_region=CHUNK2_REGION)
+        project(1, whole, nc.scalar.copy, 2)
+        quantise_w1(3, 1, 1, bf_region=CHUNK3_REGION, codes_region=W2_REGION)
+        interpolate(1, 0, 2, (CHUNK2_REGION, CHUNK3_REGION))
+        project(2, whole, nc.scalar.copy, 3)
+        project(3, whole, nc.scalar.copy, 4)
         interpolate(2, 0, 1)
         difference(0, 2, 0, 3)
         difference(0, 2, 1, 4)
@@ -253,11 +249,11 @@ def tile_picked_zwarp_abs_po_kernel(
         difference(2, 1, 1, 1)
         interpolate(3, 1, 1)
         quantise_w2()
-        quantise_z(0, 5)
+        quantise_z(0, nc.vector.tensor_copy, 5)
         difference(3, 1, 1, 2)
-        quantise_z(1, 0)
-        second_layer(0, 6)
-        second_layer_split(1, 7, 3)
+        quantise_z(1, nc.scalar.copy, 0)
+        output_one_bank(0, 6)
+        output_two_banks(1, 7, 3)
         for q in range(4):
             queue = nc.scalar if q % 2 else nc.sync
             queue.dma_start(out_2[0, 4 * q : 4 * q + 4, :].bitcast(I32), y_scales[32 * q : 32 * q + 4, :].bitcast(I32))

@@ -16,12 +16,8 @@ ACT = mybir.ActivationFunctionType
 P = 128
 K, T, S, V, H, N = 1024, 1024, 512, 256, 512, 512
 PASS = 512
+RAW11, BF0, CODES1, RAW30, RAW31, CODES0, RAW21 = 0, 4096, 6144, 8192, 12288, 18432, 20480
 FLOPS = 2 * K * H * S + 2 * H * N * V
-
-CHUNK2_REGION = 0
-CHUNK3_REGION = 1024
-W2_REGION = 2048
-W2_PIECES = 4
 
 
 def tile_picked_zwarp_abs_po_kernel(
@@ -42,96 +38,99 @@ def tile_picked_zwarp_abs_po_kernel(
 
         offs_sb = lists.tile([P, S // 16], U16, name="offs_sb")
         pos_sb = [lists.tile([P, V // 16], U16, name="pos_sb%d" % d) for d in range(2)]
-        nc.sync.dma_start(offs_sb[:], offs)
-        nc.sync.dma_start(pos_sb[0][:], pos1)
-
         xw_all = [tile([P, T], I32, "xw_all%d" % o) for o in range(2)]
+        xs_all = tile([P, T], U8, "xs_all")
+        gate_rows = tile([P, P], F32, "gate_rows")
+        w1_raw = {(c, o): tile([P, 4, P], F32, "w1_raw%d%d" % (c, o), {(1, 1): RAW11, (2, 1): RAW21, (3, 0): RAW30, (3, 1): RAW31}.get((c, o))) for c in range(4) for o in range(2)}
 
         def load_words(o):
             nc.sync.dma_start(xw_all[o][:], x_words[o].rearrange("p c r -> p (c r)").bitcast(I32))
 
-        load_words(0)
+        def load_w1(c, passes=(0, 1)):
+            for o in passes:
+                rows = w1[PASS * o : PASS * (o + 1), P * c : P * (c + 1)]
+                nc.sync.dma_start(w1_raw[c, o][:], rows.rearrange("(p j) c -> p j c", j=4))
 
-        gate_rows = tile([P, P], F32, "gate_rows")
-        nc.gpsimd.memset(gate_rows[:], 0.0)
-        nc.sync.dma_start(gate_rows[0:4, :], gate[:, 0, :].rearrange("d (h v) -> d h v", h=2))
-
-        xs_all = tile([P, T], U8, "xs_all")
+        nc.scalar.dma_start(gate_rows[:], gate.rearrange("d (r s) (h v) -> (d r) s h v", s=4, h=2)[:, 0])
         nc.vector.memset(xs_all[:].bitcast(I32), 0)
+        nc.sync.dma_start(offs_sb[:], offs)
+        load_words(0)
         for q in range(4):
             nc.sync.dma_start(xs_all[32 * q : 32 * q + 8, :].bitcast(I32), x_scales[:, 4 * q : 4 * q + 4, :].bitcast(I32))
-
-        w1_raw = {}
-
-        def load_w1(c0, chunks, o):
-            raw = tile([P, 4, P * chunks], F32, "w1_raw%d%d" % (c0, o))
-            rows = w1[PASS * o : PASS * (o + 1), P * c0 : P * (c0 + chunks)]
-            nc.sync.dma_start(raw[:], rows.rearrange("(p j) c -> p j c", j=4))
-            for b in range(chunks):
-                w1_raw[c0 + b, o] = (raw, P * b)
-
+        load_w1(0)
         load_words(1)
-        load_w1(0, 1, 0)
-        load_w1(0, 1, 1)
+        load_w1(1)
+        nc.sync.dma_start(pos_sb[0][:], pos1)
         nc.sync.dma_start(pos_sb[1][:], pos2)
-        load_w1(1, 1, 0)
-        load_w1(1, 1, 1)
-        load_w1(2, 2, 0)
-        load_w1(2, 2, 1)
+        load_w1(2)
+        load_w1(3)
         ref_sb = tile([P, 4, V], F32, "ref_sb")
+        w2_raw = [tile([P, 4, N // 2], F32, "w2_raw%d" % g, RAW30 if g else None) for g in range(2)]
+
+        def load_w2(g):
+            nc.sync.dma_start(w2_raw[g][:], w2[:, g * N // 2 : (g + 1) * N // 2].rearrange("(p j) m -> p j m", j=4))
+
+        load_w2(0)
         nc.sync.dma_start(ref_sb[:], ref.rearrange("(c p) v -> p c v", p=P))
-        w2_raw = tile([P, 4, N], F32, "w2_raw")
-        nc.sync.dma_start(w2_raw[:], w2.rearrange("(p j) m -> p j m", j=4))
+        load_w2(1)
 
         ident = tile([P, P], F32, "ident")
         make_identity(nc, ident[:])
 
-        nc.tensor.transpose(banks[5][:, 0:P], gate_rows[:], ident[:])
+        nc.tensor.transpose(banks[6][:, 0:P], gate_rows[:], ident[:])
         gate_cols = tile([P, 4], F32, "gate_cols")
-        nc.scalar.activation(gate_cols[:], banks[5][:, 0:4], ACT.Copy, scale=-1.0)
+        nc.scalar.activation(gate_cols[:].rearrange("p (d h) -> p d h", d=2), banks[6][:, 0:P].rearrange("p (d r h) -> p d r h", d=2, h=2)[:, :, 0, :], ACT.Copy, scale=-1.0)
         for n in range(4):
-            nc.tensor.transpose(banks[6][:, P * n : P * (n + 1)], gate_cols[:, n : n + 1].to_broadcast([P, P]), ident[:])
+            nc.tensor.transpose(banks[7][:, P * n : P * (n + 1)], gate_cols[:, n : n + 1].to_broadcast([P, P]), ident[:])
         neg_gate = tile([P, 2, V], F32, "neg_gate")
+        nc.scalar.copy(neg_gate[:].rearrange("p d v -> p (d v)"), banks[7][:])
 
         xs = tile([P, S], U8, "xs")
-        xw = [tile([P, S], U32, "xw%d" % o) for o in range(2)]
+        xw = [tile([P, S], U32, "xw%d" % o, BF0 if o else None) for o in range(2)]
 
         def pick_words(o, cols):
             offsets = offs_sb[:, cols.start // 16 : cols.stop // 16]
             nc.vector.tensor_copy(xw[o][:, cols], xw_all[o][:].bitcast(U32).indirect(offsets))
 
-        w1_q = {}
+        w1_bf = [tile([P, 2, P, 4], BF16, "w1_bf%d" % c, (BF0, None)[c]) for c in range(2)]
+        bf_regions = {(2, 1): CODES0 - 512, (3, 0): CODES0 + 512, (3, 1): CODES1}
+        w1_bf_pass = {(c, o): tile([P, P, 4], BF16, "w1_bf%d%d" % (c, o), bf_regions.get((c, o))) for c in (2, 3) for o in range(2)}
+        w1_codes = [tile([P, 2 * P], U32, "w1_codes%d" % c, (CODES0, CODES1, None, None)[c]) for c in range(4)]
+        w1_scales = [tile([P, 2 * P], U8, "w1_scales%d" % c) for c in range(4)]
 
-        def quantise_w1(c0, chunks, o, bf_region=None, codes_region=None):
-            raw, first = w1_raw[c0, o]
-            width = P * chunks
-            grouped = tile([P, width, 4], BF16, "w1_bf%d%d" % (c0, o), bf_region)
-            nc.scalar.copy(
-                grouped[:].rearrange("p (c n) j -> p c j n", n=4),
-                raw[:, :, first : first + width].rearrange("p j (c n) -> p c j n", n=4),
+        def round_w1(c, o, copy):
+            grouped = w1_bf_pass[c, o][:] if c >= 2 else w1_bf[c][:, o]
+            copy(
+                grouped.rearrange("p (c n) j -> p c j n", n=4),
+                w1_raw[c, o][:].rearrange("p j (c n) -> p c j n", n=4),
             )
-            codes = tile([P, width], U32, "w1_codes%d%d" % (c0, o), codes_region)
-            scales = tile([P, width], U8, "w1_scales%d%d" % (c0, o))
-            nc.vector.quantize_mx(codes[:].bitcast(FP8X4), scales[:], grouped[:].rearrange("p c j -> p (c j)"))
-            for b in range(chunks):
-                cols = slice(b * P, (b + 1) * P)
-                w1_q[c0 + b, o] = (codes[:, cols].bitcast(FP8X4), scales[:, cols])
 
-        f = [tile([P, S], F32, "f%d" % c) for c in range(4)]
+        def quantise_w1(c, o0=0, o1=2):
+            m = slice(P * o0, P * o1)
+            grouped = w1_bf_pass[c, o0][:].rearrange("p c j -> p (c j)") if c >= 2 else w1_bf[c][:].rearrange("p o c j -> p (o c j)")
+            nc.vector.quantize_mx(w1_codes[c][:, m].bitcast(FP8X4), w1_scales[c][:, m], grouped)
 
-        def project(c, cols, copy, bank):
+        f = [tile([P, S], F32, "f%d" % c, (RAW11, RAW21 + 1024, None, None)[c]) for c in range(4)]
+
+        def multiply_w1(c, o, cols, bank):
             acc = banks[bank][:, 0 : cols.stop - cols.start]
+            m = slice(P * o, P * (o + 1))
+            nc.tensor.matmul_mx(acc, w1_codes[c][:, m].bitcast(FP8X4), w1_scales[c][:, m], xw[o][:, cols].bitcast(FP8X4), xs[4 * o : P, cols], start=(o == 0), stop=(o == 1))
+
+        def copy_f(c, cols, bank):
+            nc.scalar.copy(f[c][:, cols], banks[bank][:, 0 : cols.stop - cols.start])
+
+        def project(c, cols, bank):
             for o in range(2):
-                codes, scales = w1_q[c, o]
-                nc.tensor.matmul_mx(acc, codes, scales, xw[o][:, cols].bitcast(FP8X4), xs[4 * o : P, cols], start=(o == 0), stop=(o == 1))
-            copy(f[c][:, cols], acc)
+                multiply_w1(c, o, cols, bank)
+            copy_f(c, cols, bank)
 
         terms = {}
 
-        def interpolate(c, h0, halves, regions=(None, None)):
+        def interpolate(c, h0, halves, corners=(0, 1)):
             cols = slice(P * h0, P * (h0 + halves))
-            for d in range(2):
-                term = tile([P, P * halves], F32, "term%d%d%d" % (c, h0, d), regions[d])
+            for d in corners:
+                term = tile([P, P * halves], F32, "term%d%d%d" % (c, h0, d), {(0, 1): RAW21, (1, 1): RAW31}.get((c, d)))
                 window = f[c][:].indirect(pos_sb[d][:, cols.start // 16 : cols.stop // 16])
                 nc.vector.tensor_tensor(term[:], window, neg_gate[:, d, cols], MULT)
                 for b in range(halves):
@@ -139,16 +138,17 @@ def tile_picked_zwarp_abs_po_kernel(
 
         z_t = [tile([P, H], BF16, "z_t%d" % h) for h in range(2)]
 
-        def difference(c0, chunks, h, bank):
-            e_t = banks[bank][:, 0 : chunks * P].rearrange("v (b i) -> v b i", b=chunks)
-            for b in range(chunks):
-                c = c0 + b
-                parts = [terms[c, h, 0], ref_sb[:, c, P * h : P * (h + 1)], terms[c, h, 1]]
-                for n, part in enumerate(parts):
-                    nc.tensor.matmul(e_t[:, b, :], part, ident[:], start=(n == 0), stop=(n == 2), is_transpose=True)
+        def add_turned(part, bank, b, start=False, stop=False):
+            nc.tensor.matmul(banks[bank][:, P * b : P * (b + 1)], part, ident[:], start=start, stop=stop, is_transpose=True)
+
+        def ref_part(c, h):
+            return ref_sb[:, c, P * h : P * (h + 1)]
+
+        def absolute(c0, chunks, h, bank):
+            e_t = banks[bank][:, 0 : chunks * P]
             nc.scalar.activation(
                 z_t[h][:].rearrange("v (u p e) -> v u p e", u=2, e=2)[:, :, 32 * c0 : 32 * (c0 + chunks), :],
-                e_t.rearrange("v b (q u e) -> v u (b q) e", u=2, e=2),
+                e_t.rearrange("v (q u e) -> v u q e", u=2, e=2),
                 ACT.Abs,
             )
 
@@ -168,19 +168,17 @@ def tile_picked_zwarp_abs_po_kernel(
 
         w2_codes = tile([P, N], U32, "w2_codes")
         w2_scales = tile([P, N], U8, "w2_scales")
+        w2_bf = tile([P, N, 4], BF16, "w2_bf", CODES0 - 4096)
 
-        def quantise_w2():
-            grouped = tile([P, N, 4], BF16, "w2_bf", W2_REGION)
-            piece = P // W2_PIECES
-            for g in range(W2_PIECES):
-                nc.scalar.copy(
-                    grouped[:].rearrange("p (t r) j -> p r j t", t=4)[:, piece * g : piece * (g + 1)],
-                    w2_raw[:].rearrange("p j (r t) -> p r j t", t=4)[:, piece * g : piece * (g + 1)],
-                )
-            nc.vector.quantize_mx(w2_codes[:].bitcast(FP8X4), w2_scales[:], grouped[:].rearrange("p c j -> p (c j)"))
+        def round_w2(g, r0, r1, copy):
+            copy(
+                w2_bf[:].rearrange("p (t r) j -> p r j t", t=4)[:, 64 * g + r0 : 64 * g + r1],
+                w2_raw[g][:].rearrange("p j (r t) -> p r j t", t=4)[:, r0:r1],
+            )
 
         out_rows = out_0.rearrange("(r t) v -> r t v", t=4)
         out_words = out_1[0].rearrange("r c t -> r (c t)").bitcast(I32)
+        y_codes = tile([P, V], U32, "y_codes")
         y_scales = tile([P, V], U8, "y_scales")
 
         def multiply_w2(h, t, acc):
@@ -190,70 +188,93 @@ def tile_picked_zwarp_abs_po_kernel(
 
         def quantise_y(h, y_bf):
             cols = slice(P * h, P * (h + 1))
-            y_codes = tile([P, P], U32, "y_codes%d" % h)
-            nc.vector.quantize_mx(y_codes[:].bitcast(FP8X4), y_scales[:, cols], y_bf[:].rearrange("r v t -> r (v t)"))
-            nc.sync.dma_start(out_words[:, cols], y_codes[:].bitcast(I32))
+            nc.vector.quantize_mx(y_codes[:, cols].bitcast(FP8X4), y_scales[:, cols], y_bf[:].rearrange("r v t -> r (v t)"))
 
-        def output_one_bank(h, bank):
-            acc = banks[bank][:].rearrange("r (t v) -> r t v", t=4)
+        def product(h, bank_low, bank_high):
+            pairs = [banks[b][:, 0 : 2 * P].rearrange("r (t v) -> r t v", t=2) for b in (bank_low, bank_high)]
             for t in range(4):
-                multiply_w2(h, t, acc[:, t, :])
-            y = tile([P, 4, P], F32, "y%d" % h)
-            nc.scalar.copy(y[:], acc)
-            nc.sync.dma_start(out_rows[:, :, P * h : P * (h + 1)], y[:])
-            y_bf = tile([P, P, 4], BF16, "y_bf%d" % h)
-            nc.vector.tensor_copy(y_bf[:].rearrange("r (c n) t -> r c t n", n=4), y[:].rearrange("r t (c n) -> r c t n", n=4))
-            quantise_y(h, y_bf)
+                multiply_w2(h, t, pairs[t // 2][:, t % 2, :])
+            return pairs
 
-        def output_two_banks(h, bank_low, bank_high):
-            low = banks[bank_low][:, 0 : 2 * P].rearrange("r (t v) -> r t v", t=2)
-            high = banks[bank_high][:, 0 : 2 * P].rearrange("r (t v) -> r t v", t=2)
-            for t in range(4):
-                multiply_w2(h, t, (low, high)[t // 2][:, t % 2, :])
-            y = tile([P, 4, P], F32, "y%d" % h)
-            y_bf = tile([P, P, 4], BF16, "y_bf%d" % h)
-            nc.vector.tensor_copy(y_bf[:, :, 0:2], low.rearrange("r t v -> r v t"))
-            nc.scalar.copy(y[:, 2:4, :], high)
-            nc.scalar.copy(y[:, 0:2, :], low)
-            nc.sync.dma_start(out_rows[:, :, P * h : P * (h + 1)], y[:])
-            nc.vector.tensor_copy(y_bf[:, :, 2:4], y[:, 2:4, :].rearrange("r t v -> r v t"))
-            quantise_y(h, y_bf)
+        def store_y(h, u, y):
+            nc.sync.dma_start(out_rows[:, 2 * u : 2 * u + 2, P * h : P * (h + 1)], y[:])
 
-        left, right, whole = slice(0, S // 2), slice(S // 2, S), slice(0, S)
+        whole, stretches = slice(0, S), (slice(0, 256), slice(256, 384), slice(384, 512))
         pick_words(0, whole)
         nc.vector.tensor_copy(xs[:], xs_all[:].indirect(offs_sb[:]))
-        pick_words(1, left)
-        quantise_w1(0, 1, 0)
-        pick_words(1, right)
-        quantise_w1(0, 1, 1)
-        project(0, left, nc.vector.tensor_copy, 0)
-        project(0, right, nc.vector.tensor_copy, 1)
-        quantise_w1(1, 1, 0)
-        quantise_w1(1, 1, 1, codes_region=CHUNK3_REGION)
+        act, dve = nc.scalar.copy, nc.vector.tensor_copy
+        round_w1(0, 0, act)
+        round_w1(0, 1, act)
+        quantise_w1(0)
+        for cols in stretches:
+            pick_words(1, cols)
+        round_w1(1, 0, act)
+        round_w1(1, 1, act)
+        round_w1(2, 0, act)
+        for cols, bank in zip(stretches, (0, 1, 6)):
+            project(0, cols, bank)
+        quantise_w1(1)
+        quantise_w1(2, 0, 1)
+        round_w1(2, 1, act)
+        round_w1(3, 0, act)
+        project(1, whole, 2)
+        interpolate(0, 0, 2, (0,))
+        quantise_w1(2, 1, 2)
+        interpolate(0, 0, 2, (1,))
+        quantise_w1(3, 0, 1)
+        round_w1(3, 1, act)
+        project(2, whole, 3)
+        round_w2(0, 0, 32, act)
+        multiply_w1(3, 0, whole, 0)
         for d in range(2):
-            nc.scalar.copy(neg_gate[:, d, :], banks[6][:, V * d : V * (d + 1)])
-        interpolate(0, 0, 2)
-        quantise_w1(2, 2, 0)
-        quantise_w1(2, 1, 1, bf_region=CHUNK2_REGION)
-        project(1, whole, nc.scalar.copy, 2)
-        quantise_w1(3, 1, 1, bf_region=CHUNK3_REGION, codes_region=W2_REGION)
-        interpolate(1, 0, 2, (CHUNK2_REGION, CHUNK3_REGION))
-        project(2, whole, nc.scalar.copy, 3)
-        project(3, whole, nc.scalar.copy, 4)
-        interpolate(2, 0, 1)
-        difference(0, 2, 0, 3)
-        difference(0, 2, 1, 4)
-        interpolate(3, 0, 1)
-        difference(2, 2, 0, 0)
-        interpolate(2, 1, 1)
-        difference(2, 1, 1, 1)
-        interpolate(3, 1, 1)
-        quantise_w2()
-        quantise_z(0, nc.vector.tensor_copy, 5)
-        difference(3, 1, 1, 2)
-        quantise_z(1, nc.scalar.copy, 0)
-        output_one_bank(0, 6)
-        output_two_banks(1, 7, 3)
+            for h in range(2):
+                add_turned(terms[0, h, d], 4 + h, 0, start=(d == 0))
+        interpolate(1, 0, 2, (0,))
+        quantise_w1(3, 1, 2)
+        multiply_w1(3, 1, whole, 0)
+        interpolate(1, 0, 2, (1,))
+        for d in range(2):
+            for h in range(2):
+                add_turned(terms[1, h, d], 4 + h, 1)
+        round_w2(0, 32, 64, act)
+        copy_f(3, whole, 0)
+        round_w2(1, 0, 64, act)
+        interpolate(2, 0, 2, (0,))
+        for h in range(2):
+            add_turned(terms[2, h, 0], 4 + h, 2)
+        for h, bank in ((0, 0), (1, 3)):
+            interpolate(2, h, 1, (1,))
+            for c in range(3):
+                add_turned(ref_part(c, h), 4 + h, c)
+            add_turned(terms[2, h, 1], 4 + h, 2, stop=True)
+            absolute(0, 3, h, 4 + h)
+            add_turned(ref_part(3, h), bank, 0, start=True)
+            interpolate(3, h, 1)
+            for d in range(2):
+                add_turned(terms[3, h, d], bank, 0, stop=(d == 1))
+            absolute(3, 1, h, bank)
+        nc.vector.quantize_mx(w2_codes[:].bitcast(FP8X4), w2_scales[:], w2_bf[:].rearrange("p c j -> p (c j)"))
+        quantise_z(0, dve, 1)
+        quantise_z(1, act, 2)
+        y_bf = [tile([P, P, 4], BF16, "y_bf%d" % h) for h in range(2)]
+        low, high = product(0, 6, 7)
+        y0 = tile([P, 4, P], F32, "y0")
+        dve(y_bf[0][:, :, 0:2], low.rearrange("r t v -> r v t"))
+        act(y0[:, 2:4, :], high)
+        act(y0[:, 0:2, :], low)
+        nc.sync.dma_start(out_rows[:, :, 0:P], y0[:])
+        dve(y_bf[0][:, :, 2:4], y0[:, 2:4, :].rearrange("r t v -> r v t"))
+        low, high = product(1, 4, 5)
+        y1 = [tile([P, 2, P], F32, "y1%d" % u) for u in range(2)]
+        dve(y_bf[1][:, :, 0:2], low.rearrange("r t v -> r v t"))
+        act(y_bf[1][:, :, 2:4], high.rearrange("r t v -> r v t"))
+        quantise_y(0, y_bf[0])
+        dve(y1[0][:], low)
+        store_y(1, 0, y1[0])
+        act(y1[1][:], high)
+        store_y(1, 1, y1[1])
+        quantise_y(1, y_bf[1])
+        nc.sync.dma_start(out_words, y_codes[:].bitcast(I32))
         for q in range(4):
             queue = nc.scalar if q % 2 else nc.sync
             queue.dma_start(out_2[0, 4 * q : 4 * q + 4, :].bitcast(I32), y_scales[32 * q : 32 * q + 4, :].bitcast(I32))

@@ -16,7 +16,8 @@ ACT = mybir.ActivationFunctionType
 P = 128
 K, T, S, V, H, N = 1024, 1024, 512, 256, 512, 512
 PASS = 512
-RAW11, BF0, CODES1, RAW30, RAW31, CODES0, RAW21 = 0, 4096, 6144, 8192, 12288, 18432, 20480
+CODES0, RAW31, RAW30, RAW21, F3 = 0, 2048, 4096, 6144, 9216
+GATE = 13312
 FLOPS = 2 * K * H * S + 2 * H * N * V
 
 
@@ -41,76 +42,71 @@ def tile_picked_zwarp_abs_po_kernel(
         xw_all = [tile([P, T], I32, "xw_all%d" % o) for o in range(2)]
         xs_all = tile([P, T], U8, "xs_all")
         gate_rows = tile([P, P], F32, "gate_rows")
-        w1_raw = {(c, o): tile([P, 4, P], F32, "w1_raw%d%d" % (c, o), {(1, 1): RAW11, (2, 1): RAW21, (3, 0): RAW30, (3, 1): RAW31}.get((c, o))) for c in range(4) for o in range(2)}
+        w1_raw = {}
 
         def load_words(o):
             nc.sync.dma_start(xw_all[o][:], x_words[o].rearrange("p c r -> p (c r)").bitcast(I32))
 
-        def load_w1(c, passes=(0, 1)):
-            for o in passes:
-                rows = w1[PASS * o : PASS * (o + 1), P * c : P * (c + 1)]
-                nc.sync.dma_start(w1_raw[c, o][:], rows.rearrange("(p j) c -> p j c", j=4))
+        def load_w1(c, o):
+            raw = tile([P, 4, P], F32, "w1_raw%d%d" % (c, o), {(2, 1): RAW21, (3, 0): RAW30, (3, 1): RAW31}.get((c, o)))
+            rows = w1[PASS * o : PASS * (o + 1), P * c : P * (c + 1)]
+            nc.sync.dma_start(raw[:], rows.rearrange("(p j) c -> p j c", j=4))
+            w1_raw[c, o] = raw[:]
 
-        nc.scalar.dma_start(gate_rows[:], gate.rearrange("d (r s) (h v) -> (d r) s h v", s=4, h=2)[:, 0])
+        nc.gpsimd.memset(gate_rows[:], 0.0)
+        nc.scalar.dma_start(gate_rows[0:4, :], gate[:, 0, :].rearrange("d (h v) -> d h v", h=2))
         nc.vector.memset(xs_all[:].bitcast(I32), 0)
-        nc.sync.dma_start(offs_sb[:], offs)
         load_words(0)
+        nc.sync.dma_start(offs_sb[:], offs)
         for q in range(4):
             nc.sync.dma_start(xs_all[32 * q : 32 * q + 8, :].bitcast(I32), x_scales[:, 4 * q : 4 * q + 4, :].bitcast(I32))
-        load_w1(0)
         load_words(1)
-        load_w1(1)
-        nc.sync.dma_start(pos_sb[0][:], pos1)
-        nc.sync.dma_start(pos_sb[1][:], pos2)
-        load_w1(2)
-        load_w1(3)
+        for c in range(4):
+            load_w1(c, 0)
+            if c == 2:
+                nc.sync.dma_start(pos_sb[1][:], pos2)
+            load_w1(c, 1)
+            if c == 1:
+                nc.sync.dma_start(pos_sb[0][:], pos1)
         ref_sb = tile([P, 4, V], F32, "ref_sb")
-        w2_raw = [tile([P, 4, N // 2], F32, "w2_raw%d" % g, RAW30 if g else None) for g in range(2)]
-
-        def load_w2(g):
-            nc.sync.dma_start(w2_raw[g][:], w2[:, g * N // 2 : (g + 1) * N // 2].rearrange("(p j) m -> p j m", j=4))
-
-        load_w2(0)
         nc.sync.dma_start(ref_sb[:], ref.rearrange("(c p) v -> p c v", p=P))
-        load_w2(1)
+        w2_raw = tile([P, 4, N], F32, "w2_raw")
+        nc.sync.dma_start(w2_raw[:], w2.rearrange("(p j) m -> p j m", j=4))
 
         ident = tile([P, P], F32, "ident")
         make_identity(nc, ident[:])
 
         nc.tensor.transpose(banks[6][:, 0:P], gate_rows[:], ident[:])
-        gate_cols = tile([P, 4], F32, "gate_cols")
-        nc.scalar.activation(gate_cols[:].rearrange("p (d h) -> p d h", d=2), banks[6][:, 0:P].rearrange("p (d r h) -> p d r h", d=2, h=2)[:, :, 0, :], ACT.Copy, scale=-1.0)
+        gate_cols = tile([P, 768], F32, "gate_cols", GATE)
+        nc.scalar.activation(gate_cols[:, 0:4], banks[6][:, 0:4], ACT.Copy, scale=-1.0)
         for n in range(4):
             nc.tensor.transpose(banks[7][:, P * n : P * (n + 1)], gate_cols[:, n : n + 1].to_broadcast([P, P]), ident[:])
         neg_gate = tile([P, 2, V], F32, "neg_gate")
         nc.scalar.copy(neg_gate[:].rearrange("p d v -> p (d v)"), banks[7][:])
 
         xs = tile([P, S], U8, "xs")
-        xw = [tile([P, S], U32, "xw%d" % o, BF0 if o else None) for o in range(2)]
+        xw = [tile([P, S], U32, "xw%d" % o) for o in range(2)]
 
         def pick_words(o, cols):
             offsets = offs_sb[:, cols.start // 16 : cols.stop // 16]
             nc.vector.tensor_copy(xw[o][:, cols], xw_all[o][:].bitcast(U32).indirect(offsets))
 
-        w1_bf = [tile([P, 2, P, 4], BF16, "w1_bf%d" % c, (BF0, None)[c]) for c in range(2)]
-        bf_regions = {(2, 1): CODES0 - 512, (3, 0): CODES0 + 512, (3, 1): CODES1}
-        w1_bf_pass = {(c, o): tile([P, P, 4], BF16, "w1_bf%d%d" % (c, o), bf_regions.get((c, o))) for c in (2, 3) for o in range(2)}
-        w1_codes = [tile([P, 2 * P], U32, "w1_codes%d" % c, (CODES0, CODES1, None, None)[c]) for c in range(4)]
+        bf_regions = {(0, 0): GATE, (0, 1): GATE + 1024, (1, 0): GATE + 2048, (1, 1): GATE + 1024, (2, 0): GATE + 1024, (2, 1): CODES0 + 512, (3, 0): RAW21, (3, 1): CODES0 + 1024}
+        w1_bf = {(c, o): tile([P, P, 4], BF16, "w1_bf%d%d" % (c, o), bf_regions.get((c, o))) for c in range(4) for o in range(2)}
+        w1_codes = [tile([P, 2 * P], U32, "w1_codes%d" % c, CODES0 if c == 0 else None) for c in range(4)]
         w1_scales = [tile([P, 2 * P], U8, "w1_scales%d" % c) for c in range(4)]
 
         def round_w1(c, o, copy):
-            grouped = w1_bf_pass[c, o][:] if c >= 2 else w1_bf[c][:, o]
             copy(
-                grouped.rearrange("p (c n) j -> p c j n", n=4),
-                w1_raw[c, o][:].rearrange("p j (c n) -> p c j n", n=4),
+                w1_bf[c, o][:].rearrange("p (c n) j -> p c j n", n=4),
+                w1_raw[c, o].rearrange("p j (c n) -> p c j n", n=4),
             )
 
-        def quantise_w1(c, o0=0, o1=2):
-            m = slice(P * o0, P * o1)
-            grouped = w1_bf_pass[c, o0][:].rearrange("p c j -> p (c j)") if c >= 2 else w1_bf[c][:].rearrange("p o c j -> p (o c j)")
-            nc.vector.quantize_mx(w1_codes[c][:, m].bitcast(FP8X4), w1_scales[c][:, m], grouped)
+        def quantise_w1(c, o):
+            m = slice(P * o, P * (o + 1))
+            nc.vector.quantize_mx(w1_codes[c][:, m].bitcast(FP8X4), w1_scales[c][:, m], w1_bf[c, o][:].rearrange("p c j -> p (c j)"))
 
-        f = [tile([P, S], F32, "f%d" % c, (RAW11, RAW21 + 1024, None, None)[c]) for c in range(4)]
+        f = [tile([P, S], F32, "f%d" % c, (None, RAW21 + 1024, None, F3)[c]) for c in range(4)]
 
         def multiply_w1(c, o, cols, bank):
             acc = banks[bank][:, 0 : cols.stop - cols.start]
@@ -130,11 +126,23 @@ def tile_picked_zwarp_abs_po_kernel(
         def interpolate(c, h0, halves, corners=(0, 1)):
             cols = slice(P * h0, P * (h0 + halves))
             for d in corners:
-                term = tile([P, P * halves], F32, "term%d%d%d" % (c, h0, d), {(0, 1): RAW21, (1, 1): RAW31}.get((c, d)))
+                term = tile([P, P * halves], F32, "term%d%d%d" % (c, h0, d), {(1, 0, 1): RAW30, (1, 1, 1): RAW31}.get((c, h0, d)))
                 window = f[c][:].indirect(pos_sb[d][:, cols.start // 16 : cols.stop // 16])
                 nc.vector.tensor_tensor(term[:], window, neg_gate[:, d, cols], MULT)
                 for b in range(halves):
                     terms[c, h0 + b, d] = term[:, P * b : P * (b + 1)]
+
+        def fetch(c, h0, halves):
+            cols = slice(P * h0, P * (h0 + halves))
+            picked = tile([P, P * halves], F32, "picked%d%d" % (c, h0))
+            nc.scalar.activation(picked[:], f[c][:].indirect(pos_sb[1][:, cols.start // 16 : cols.stop // 16]), ACT.Copy)
+            return picked
+
+        def weigh(c, h0, halves, picked):
+            term = tile([P, P * halves], F32, "term%d%d1" % (c, h0))
+            nc.vector.tensor_tensor(term[:], picked[:], neg_gate[:, 1, P * h0 : P * (h0 + halves)], MULT)
+            for b in range(halves):
+                terms[c, h0 + b, 1] = term[:, P * b : P * (b + 1)]
 
         z_t = [tile([P, H], BF16, "z_t%d" % h) for h in range(2)]
 
@@ -144,8 +152,8 @@ def tile_picked_zwarp_abs_po_kernel(
         def ref_part(c, h):
             return ref_sb[:, c, P * h : P * (h + 1)]
 
-        def absolute(c0, chunks, h, bank):
-            e_t = banks[bank][:, 0 : chunks * P]
+        def absolute(c0, chunks, h, bank, b0=0):
+            e_t = banks[bank][:, b0 * P : (b0 + chunks) * P]
             nc.scalar.activation(
                 z_t[h][:].rearrange("v (u p e) -> v u p e", u=2, e=2)[:, :, 32 * c0 : 32 * (c0 + chunks), :],
                 e_t.rearrange("v (q u e) -> v u q e", u=2, e=2),
@@ -168,17 +176,16 @@ def tile_picked_zwarp_abs_po_kernel(
 
         w2_codes = tile([P, N], U32, "w2_codes")
         w2_scales = tile([P, N], U8, "w2_scales")
-        w2_bf = tile([P, N, 4], BF16, "w2_bf", CODES0 - 4096)
+        w2_bf = tile([P, N, 4], BF16, "w2_bf", F3)
 
-        def round_w2(g, r0, r1, copy):
-            copy(
-                w2_bf[:].rearrange("p (t r) j -> p r j t", t=4)[:, 64 * g + r0 : 64 * g + r1],
-                w2_raw[g][:].rearrange("p j (r t) -> p r j t", t=4)[:, r0:r1],
-            )
+        def quantise_w2():
+            nc.vector.tensor_copy(w2_bf[:].rearrange("p (t r) j -> p r j t", t=4), w2_raw[:].rearrange("p j (r t) -> p r j t", t=4))
+            for t in range(4):
+                m = slice(P * t, P * (t + 1))
+                nc.vector.quantize_mx(w2_codes[:, m].bitcast(FP8X4), w2_scales[:, m], w2_bf[:, m].rearrange("p r j -> p (r j)"))
 
         out_rows = out_0.rearrange("(r t) v -> r t v", t=4)
         out_words = out_1[0].rearrange("r c t -> r (c t)").bitcast(I32)
-        y_codes = tile([P, V], U32, "y_codes")
         y_scales = tile([P, V], U8, "y_scales")
 
         def multiply_w2(h, t, acc):
@@ -188,93 +195,105 @@ def tile_picked_zwarp_abs_po_kernel(
 
         def quantise_y(h, y_bf):
             cols = slice(P * h, P * (h + 1))
-            nc.vector.quantize_mx(y_codes[:, cols].bitcast(FP8X4), y_scales[:, cols], y_bf[:].rearrange("r v t -> r (v t)"))
+            y_codes = tile([P, P], U32, "y_codes%d" % h)
+            nc.vector.quantize_mx(y_codes[:].bitcast(FP8X4), y_scales[:, cols], y_bf[:].rearrange("r v t -> r (v t)"))
+            nc.sync.dma_start(out_words[:, cols], y_codes[:].bitcast(I32))
 
-        def product(h, bank_low, bank_high):
-            pairs = [banks[b][:, 0 : 2 * P].rearrange("r (t v) -> r t v", t=2) for b in (bank_low, bank_high)]
+        def output_one_bank(h, bank):
+            acc = banks[bank][:].rearrange("r (t v) -> r t v", t=4)
             for t in range(4):
-                multiply_w2(h, t, pairs[t // 2][:, t % 2, :])
-            return pairs
+                multiply_w2(h, t, acc[:, t, :])
+            y = tile([P, 4, P], F32, "y%d" % h)
+            nc.scalar.copy(y[:], acc)
+            nc.sync.dma_start(out_rows[:, :, P * h : P * (h + 1)], y[:])
+            y_bf = tile([P, P, 4], BF16, "y_bf%d" % h)
+            nc.vector.tensor_copy(y_bf[:].rearrange("r (c n) t -> r c t n", n=4), y[:].rearrange("r t (c n) -> r c t n", n=4))
+            quantise_y(h, y_bf)
 
-        def store_y(h, u, y):
-            nc.sync.dma_start(out_rows[:, 2 * u : 2 * u + 2, P * h : P * (h + 1)], y[:])
+        def output_two_banks(h, bank_low, bank_high):
+            low = banks[bank_low][:, 0 : 2 * P].rearrange("r (t v) -> r t v", t=2)
+            high = banks[bank_high][:, 0 : 2 * P].rearrange("r (t v) -> r t v", t=2)
+            for t in range(4):
+                multiply_w2(h, t, (low, high)[t // 2][:, t % 2, :])
+            y = tile([P, 4, P], F32, "y%d" % h)
+            y_bf = tile([P, P, 4], BF16, "y_bf%d" % h)
+            nc.vector.tensor_copy(y_bf[:, :, 0:2], low.rearrange("r t v -> r v t"))
+            nc.scalar.copy(y[:, 2:4, :], high)
+            nc.scalar.copy(y[:, 0:2, :], low)
+            nc.sync.dma_start(out_rows[:, :, P * h : P * (h + 1)], y[:])
+            nc.vector.tensor_copy(y_bf[:, :, 2:4], y[:, 2:4, :].rearrange("r t v -> r v t"))
+            quantise_y(h, y_bf)
 
-        whole, stretches = slice(0, S), (slice(0, 256), slice(256, 384), slice(384, 512))
+        left, right, whole = slice(0, S // 2), slice(S // 2, S), slice(0, S)
+        act, dve = nc.scalar.copy, nc.vector.tensor_copy
         pick_words(0, whole)
         nc.vector.tensor_copy(xs[:], xs_all[:].indirect(offs_sb[:]))
-        act, dve = nc.scalar.copy, nc.vector.tensor_copy
+        for n in range(2):
+            nc.tensor.matmul_mx(banks[7][:], xw[0][:, 0:P].bitcast(FP8X4), xs[:, 0:P], xw[0][:].bitcast(FP8X4), xs[:], start=True, stop=True)
+        pick_words(1, whole)
         round_w1(0, 0, act)
         round_w1(0, 1, act)
-        quantise_w1(0)
-        for cols in stretches:
-            pick_words(1, cols)
+        quantise_w1(0, 0)
         round_w1(1, 0, act)
-        round_w1(1, 1, act)
-        round_w1(2, 0, act)
-        for cols, bank in zip(stretches, (0, 1, 6)):
-            project(0, cols, bank)
-        quantise_w1(1)
-        quantise_w1(2, 0, 1)
+        quantise_w1(0, 1)
+        round_w1(1, 1, dve)
+        quantise_w1(1, 0)
+        quantise_w1(1, 1)
+        project(0, left, 0)
+        project(0, right, 1)
+        round_w1(2, 0, dve)
         round_w1(2, 1, act)
-        round_w1(3, 0, act)
         project(1, whole, 2)
         interpolate(0, 0, 2, (0,))
-        quantise_w1(2, 1, 2)
+        quantise_w1(2, 0)
         interpolate(0, 0, 2, (1,))
-        quantise_w1(3, 0, 1)
+        quantise_w1(2, 1)
+        round_w1(3, 0, act)
         round_w1(3, 1, act)
         project(2, whole, 3)
-        round_w2(0, 0, 32, act)
-        multiply_w1(3, 0, whole, 0)
         for d in range(2):
             for h in range(2):
-                add_turned(terms[0, h, d], 4 + h, 0, start=(d == 0))
+                add_turned(terms[0, h, d], 4, 2 * h, start=(d == 0 and h == 0))
         interpolate(1, 0, 2, (0,))
-        quantise_w1(3, 1, 2)
-        multiply_w1(3, 1, whole, 0)
-        interpolate(1, 0, 2, (1,))
-        for d in range(2):
-            for h in range(2):
-                add_turned(terms[1, h, d], 4 + h, 1)
-        round_w2(0, 32, 64, act)
-        copy_f(3, whole, 0)
-        round_w2(1, 0, 64, act)
-        interpolate(2, 0, 2, (0,))
+        quantise_w1(3, 0)
+        multiply_w1(3, 0, left, 0)
+        multiply_w1(3, 0, right, 1)
+        interpolate(1, 0, 1, (1,))
+        quantise_w1(3, 1)
+        multiply_w1(3, 1, left, 0)
+        multiply_w1(3, 1, right, 1)
+        interpolate(1, 1, 1, (1,))
+        picked2 = fetch(2, 1, 1)
+        copy_f(3, left, 0)
+        copy_f(3, right, 1)
+        picked = [fetch(3, h, 1) for h in range(2)]
+        for d in (1, 0):
+            for h in (1, 0):
+                add_turned(terms[1, h, d], 4, 2 * h + 1)
         for h in range(2):
-            add_turned(terms[2, h, 0], 4 + h, 2)
-        for h, bank in ((0, 0), (1, 3)):
-            interpolate(2, h, 1, (1,))
-            for c in range(3):
-                add_turned(ref_part(c, h), 4 + h, c)
-            add_turned(terms[2, h, 1], 4 + h, 2, stop=True)
-            absolute(0, 3, h, 4 + h)
-            add_turned(ref_part(3, h), bank, 0, start=True)
-            interpolate(3, h, 1)
+            for c in range(2):
+                add_turned(ref_part(c, h), 4, 2 * h + c, stop=(c == 1 and h == 1))
+        for h in range(2):
+            absolute(0, 2, h, 4, 2 * h)
+        interpolate(2, 0, 2, (0,))
+        interpolate(2, 0, 1, (1,))
+        weigh(2, 1, 1, picked2)
+        for h, bank in ((0, 2), (1, 5)):
             for d in range(2):
-                add_turned(terms[3, h, d], bank, 0, stop=(d == 1))
-            absolute(3, 1, h, bank)
-        nc.vector.quantize_mx(w2_codes[:].bitcast(FP8X4), w2_scales[:], w2_bf[:].rearrange("p c j -> p (c j)"))
-        quantise_z(0, dve, 1)
-        quantise_z(1, act, 2)
-        y_bf = [tile([P, P, 4], BF16, "y_bf%d" % h) for h in range(2)]
-        low, high = product(0, 6, 7)
-        y0 = tile([P, 4, P], F32, "y0")
-        dve(y_bf[0][:, :, 0:2], low.rearrange("r t v -> r v t"))
-        act(y0[:, 2:4, :], high)
-        act(y0[:, 0:2, :], low)
-        nc.sync.dma_start(out_rows[:, :, 0:P], y0[:])
-        dve(y_bf[0][:, :, 2:4], y0[:, 2:4, :].rearrange("r t v -> r v t"))
-        low, high = product(1, 4, 5)
-        y1 = [tile([P, 2, P], F32, "y1%d" % u) for u in range(2)]
-        dve(y_bf[1][:, :, 0:2], low.rearrange("r t v -> r v t"))
-        act(y_bf[1][:, :, 2:4], high.rearrange("r t v -> r v t"))
-        quantise_y(0, y_bf[0])
-        dve(y1[0][:], low)
-        store_y(1, 0, y1[0])
-        act(y1[1][:], high)
-        store_y(1, 1, y1[1])
-        quantise_y(1, y_bf[1])
-        nc.sync.dma_start(out_words, y_codes[:].bitcast(I32))
+                add_turned(terms[2, h, d], bank, 0, start=(d == 0))
+            for c in range(2):
+                add_turned(ref_part(2 + c, h), bank, c)
+        for h, bank in ((0, 2), (1, 5)):
+            weigh(3, h, 1, picked[h])
+            interpolate(3, h, 1, (0,))
+            for d in (1, 0):
+                add_turned(terms[3, h, d], bank, 1, stop=(d == 0))
+            absolute(2, 2, h, bank)
+        quantise_w2()
+        quantise_z(0, act, 0)
+        quantise_z(1, act, 1)
+        output_one_bank(0, 3)
+        output_two_banks(1, 7, 4)
         for q in range(4):
             queue = nc.scalar if q % 2 else nc.sync
             queue.dma_start(out_2[0, 4 * q : 4 * q + 4, :].bitcast(I32), y_scales[32 * q : 32 * q + 4, :].bitcast(I32))

@@ -16,8 +16,8 @@ ACT = mybir.ActivationFunctionType
 P = 128
 K, T, S, V, H, N = 1024, 1024, 512, 256, 512, 512
 PASS = 512
-CODES0, RAW31, RAW30, RAW21, F3 = 0, 2048, 4096, 6144, 9216
-GATE = 13312
+CODES0, RAW31, RAW30, RAW21, F3 = 0, 2048, 4096, 6144, 10240
+GATE = 14336
 FLOPS = 2 * K * H * S + 2 * H * N * V
 
 
@@ -176,13 +176,16 @@ def tile_picked_zwarp_abs_po_kernel(
 
         w2_codes = tile([P, N], U32, "w2_codes")
         w2_scales = tile([P, N], U8, "w2_scales")
-        w2_bf = tile([P, N, 4], BF16, "w2_bf", F3)
+        w2_bf = [tile([P, 2 * P, 4], BF16, "w2_bf%d" % a, F3 - 1024 + 2048 * a) for a in range(2)]
 
-        def quantise_w2():
-            nc.vector.tensor_copy(w2_bf[:].rearrange("p (t r) j -> p r j t", t=4), w2_raw[:].rearrange("p j (r t) -> p r j t", t=4))
-            for t in range(4):
-                m = slice(P * t, P * (t + 1))
-                nc.vector.quantize_mx(w2_codes[:, m].bitcast(FP8X4), w2_scales[:, m], w2_bf[:, m].rearrange("p r j -> p (r j)"))
+        def round_w2(a):
+            dealt = w2_raw[:].rearrange("p j (r t) -> p r j t", t=4)
+            nc.vector.tensor_copy(w2_bf[a][:].rearrange("p (t r) j -> p r j t", t=2), dealt[:, :, :, 2 * a : 2 * a + 2])
+
+        def quantise_w2(t0, slots):
+            m = slice(P * t0, P * (t0 + slots))
+            rounded = w2_bf[t0 // 2][:, P * (t0 % 2) : P * (t0 % 2 + slots), :]
+            nc.vector.quantize_mx(w2_codes[:, m].bitcast(FP8X4), w2_scales[:, m], rounded.rearrange("p r j -> p (r j)"))
 
         out_rows = out_0.rearrange("(r t) v -> r t v", t=4)
         out_words = out_1[0].rearrange("r c t -> r (c t)").bitcast(I32)
@@ -199,37 +202,27 @@ def tile_picked_zwarp_abs_po_kernel(
             nc.vector.quantize_mx(y_codes[:].bitcast(FP8X4), y_scales[:, cols], y_bf[:].rearrange("r v t -> r (v t)"))
             nc.sync.dma_start(out_words[:, cols], y_codes[:].bitcast(I32))
 
-        def output_one_bank(h, bank):
-            acc = banks[bank][:].rearrange("r (t v) -> r t v", t=4)
-            for t in range(4):
-                multiply_w2(h, t, acc[:, t, :])
-            y = tile([P, 4, P], F32, "y%d" % h)
-            nc.scalar.copy(y[:], acc)
-            nc.sync.dma_start(out_rows[:, :, P * h : P * (h + 1)], y[:])
-            y_bf = tile([P, P, 4], BF16, "y_bf%d" % h)
-            nc.vector.tensor_copy(y_bf[:].rearrange("r (c n) t -> r c t n", n=4), y[:].rearrange("r t (c n) -> r c t n", n=4))
-            quantise_y(h, y_bf)
+        y = [tile([P, 4, P], F32, "y%d" % h) for h in range(2)]
+        y_bf = [tile([P, P, 4], BF16, "y_bf%d" % h) for h in range(2)]
 
-        def output_two_banks(h, bank_low, bank_high):
-            low = banks[bank_low][:, 0 : 2 * P].rearrange("r (t v) -> r t v", t=2)
-            high = banks[bank_high][:, 0 : 2 * P].rearrange("r (t v) -> r t v", t=2)
-            for t in range(4):
-                multiply_w2(h, t, (low, high)[t // 2][:, t % 2, :])
-            y = tile([P, 4, P], F32, "y%d" % h)
-            y_bf = tile([P, P, 4], BF16, "y_bf%d" % h)
-            nc.vector.tensor_copy(y_bf[:, :, 0:2], low.rearrange("r t v -> r v t"))
-            nc.scalar.copy(y[:, 2:4, :], high)
-            nc.scalar.copy(y[:, 0:2, :], low)
-            nc.sync.dma_start(out_rows[:, :, P * h : P * (h + 1)], y[:])
-            nc.vector.tensor_copy(y_bf[:, :, 2:4], y[:, 2:4, :].rearrange("r t v -> r v t"))
-            quantise_y(h, y_bf)
+        def project_z(h, parts):
+            for slots, bank, copy in parts:
+                acc = banks[bank][:, 0 : len(slots) * P].rearrange("r (t v) -> r t v", v=P)
+                for n, t in enumerate(slots):
+                    multiply_w2(h, t, acc[:, n, :])
+                copy(y[h][:, slots.start : slots.stop, :], acc)
+            nc.sync.dma_start(out_rows[:, :, P * h : P * (h + 1)], y[h][:])
+
+        def round_y(h, slots):
+            nc.vector.tensor_copy(
+                y_bf[h][:].rearrange("r (c n) t -> r c t n", n=4)[:, :, slots, :],
+                y[h][:].rearrange("r t (c n) -> r c t n", n=4)[:, :, slots, :],
+            )
 
         left, right, whole = slice(0, S // 2), slice(S // 2, S), slice(0, S)
         act, dve = nc.scalar.copy, nc.vector.tensor_copy
         pick_words(0, whole)
         nc.vector.tensor_copy(xs[:], xs_all[:].indirect(offs_sb[:]))
-        for n in range(2):
-            nc.tensor.matmul_mx(banks[7][:], xw[0][:, 0:P].bitcast(FP8X4), xs[:, 0:P], xw[0][:].bitcast(FP8X4), xs[:], start=True, stop=True)
         pick_words(1, whole)
         round_w1(0, 0, act)
         round_w1(0, 1, act)
@@ -278,22 +271,36 @@ def tile_picked_zwarp_abs_po_kernel(
         interpolate(2, 0, 2, (0,))
         interpolate(2, 0, 1, (1,))
         weigh(2, 1, 1, picked2)
-        for h, bank in ((0, 2), (1, 5)):
-            for d in range(2):
-                add_turned(terms[2, h, d], bank, 0, start=(d == 0))
-            for c in range(2):
-                add_turned(ref_part(2 + c, h), bank, c)
-        for h, bank in ((0, 2), (1, 5)):
+        for h in range(2):
+            add_turned(terms[2, h, 0], 2, h, start=(h == 0))
+        for h in range(2):
+            add_turned(ref_part(2, h), 2, h)
+        for h in range(2):
+            add_turned(terms[2, h, 1], 2, h, stop=(h == 1))
+        for h in range(2):
+            add_turned(ref_part(3, h), h, 0, start=True)
+        for h in range(2):
+            absolute(2, 1, h, 2, h)
+        for h in range(2):
             weigh(3, h, 1, picked[h])
             interpolate(3, h, 1, (0,))
             for d in (1, 0):
-                add_turned(terms[3, h, d], bank, 1, stop=(d == 0))
-            absolute(2, 2, h, bank)
-        quantise_w2()
-        quantise_z(0, act, 0)
-        quantise_z(1, act, 1)
-        output_one_bank(0, 3)
-        output_two_banks(1, 7, 4)
+                add_turned(terms[3, h, d], h, 0, stop=(d == 0))
+            absolute(3, 1, h, h)
+        for a in range(2):
+            round_w2(a)
+        quantise_w2(0, 2)
+        quantise_w2(2, 1)
+        quantise_z(0, act, 5)
+        quantise_w2(3, 1)
+        quantise_z(1, act, 6)
+        project_z(0, ((range(0, 2), 3, act), (range(2, 4), 2, act)))
+        project_z(1, ((range(0, 2), 7, act), (range(2, 4), 4, act)))
+        round_y(0, slice(0, 4))
+        round_y(1, slice(0, 2))
+        round_y(1, slice(2, 4))
+        for h in range(2):
+            quantise_y(h, y_bf[h])
         for q in range(4):
             queue = nc.scalar if q % 2 else nc.sync
             queue.dma_start(out_2[0, 4 * q : 4 * q + 4, :].bitcast(I32), y_scales[32 * q : 32 * q + 4, :].bitcast(I32))

@@ -284,8 +284,8 @@ def tile_picked_zwarp_abs_po_kernel(
         for h in range(2):
             weigh(3, h, 1, picked[h])
             interpolate(3, h, 1, (0,))
-            for d in (1, 0):
-                add_turned(terms[3, h, d], h, 0, stop=(d == 0))
+            for d in range(2):
+                add_turned(terms[3, h, d], h, 0, stop=(d == 1))
             absolute(3, 1, h, h)
         for a in range(2):
             round_w2(a)

from contextlib import ExitStack

import concourse.mybir as mybir
from concourse.masks import make_identity

F32 = mybir.dt.float32
BF16 = mybir.dt.bfloat16
I32 = mybir.dt.int32
U32 = mybir.dt.uint32
U16 = mybir.dt.uint16
U8 = mybir.dt.uint8
FP8X4 = mybir.dt.float8_e4m3fn_x4
MULT = mybir.AluOpType.mult
ACT = mybir.ActivationFunctionType

P = 128
K, T, S, V, H, N = 1024, 1024, 512, 256, 512, 512
PASS = 512
CODES0, RAW31, RAW30, RAW21, F3 = 0, 2048, 4096, 6144, 10240
GATE = 14336
FLOPS = 2 * K * H * S + 2 * H * N * V


def tile_picked_zwarp_abs_po_kernel(
    tc, x_words, x_scales, w1, w2, gate, ref, offs, pos1, pos2, out_0, out_1, out_2
):
    nc = tc.nc
    with ExitStack() as ctx:
        lists = ctx.enter_context(tc.tile_pool(name="lists", bufs=1))
        sb = ctx.enter_context(tc.tile_pool(name="sb", bufs=1))
        overlay = ctx.enter_context(tc.tile_pool(name="overlay", bufs=1))
        psum = ctx.enter_context(tc.psum_pool(name="psum", bufs=1))
        banks = [psum.tile([P, 512], F32, name="bank%d" % b) for b in range(8)]

        def tile(shape, dtype, name, region=None):
            if region is None:
                return sb.tile(shape, dtype, name=name, align_bytes=64)
            return overlay.tile(shape, dtype, name=name, offset=region, align_bytes=64)

        offs_sb = lists.tile([P, S // 16], U16, name="offs_sb")
        pos_sb = [lists.tile([P, V // 16], U16, name="pos_sb%d" % d) for d in range(2)]
        xw_all = [tile([P, T], I32, "xw_all%d" % o) for o in range(2)]
        xs_all = tile([P, T], U8, "xs_all")
        gate_rows = tile([P, P], F32, "gate_rows")
        w1_raw = {}

        def load_words(o):
            nc.sync.dma_start(xw_all[o][:], x_words[o].rearrange("p c r -> p (c r)").bitcast(I32))

        def load_w1(c, o):
            raw = tile([P, 4, P], F32, "w1_raw%d%d" % (c, o), {(2, 1): RAW21, (3, 0): RAW30, (3, 1): RAW31}.get((c, o)))
            rows = w1[PASS * o : PASS * (o + 1), P * c : P * (c + 1)]
            nc.sync.dma_start(raw[:], rows.rearrange("(p j) c -> p j c", j=4))
            w1_raw[c, o] = raw[:]

        nc.gpsimd.memset(gate_rows[:], 0.0)
        nc.scalar.dma_start(gate_rows[0:4, :], gate[:, 0, :].rearrange("d (h v) -> d h v", h=2))
        nc.vector.memset(xs_all[:].bitcast(I32), 0)
        load_words(0)
        nc.sync.dma_start(offs_sb[:], offs)
        for q in range(4):
            nc.sync.dma_start(xs_all[32 * q : 32 * q + 8, :].bitcast(I32), x_scales[:, 4 * q : 4 * q + 4, :].bitcast(I32))
        load_words(1)
        for c in range(4):
            load_w1(c, 0)
            if c == 2:
                nc.sync.dma_start(pos_sb[1][:], pos2)
            load_w1(c, 1)
            if c == 1:
                nc.sync.dma_start(pos_sb[0][:], pos1)
        ref_sb = tile([P, 4, V], F32, "ref_sb")
        nc.sync.dma_start(ref_sb[:], ref.rearrange("(c p) v -> p c v", p=P))
        w2_raw = tile([P, 4, N], F32, "w2_raw")
        nc.sync.dma_start(w2_raw[:], w2.rearrange("(p j) m -> p j m", j=4))

        ident = tile([P, P], F32, "ident")
        make_identity(nc, ident[:])

        nc.tensor.transpose(banks[6][:, 0:P], gate_rows[:], ident[:])
        gate_cols = tile([P, 768], F32, "gate_cols", GATE)
        nc.scalar.activation(gate_cols[:, 0:4], banks[6][:, 0:4], ACT.Copy, scale=-1.0)
        for n in range(4):
            nc.tensor.transpose(banks[7][:, P * n : P * (n + 1)], gate_cols[:, n : n + 1].to_broadcast([P, P]), ident[:])
        neg_gate = tile([P, 2, V], F32, "neg_gate")
        nc.scalar.copy(neg_gate[:].rearrange("p d v -> p (d v)"), banks[7][:])

        xs = tile([P, S], U8, "xs")
        xw = [tile([P, S], U32, "xw%d" % o) for o in range(2)]

        def pick_words(o, cols):
            offsets = offs_sb[:, cols.start // 16 : cols.stop // 16]
            nc.vector.tensor_copy(xw[o][:, cols], xw_all[o][:].bitcast(U32).indirect(offsets))

        bf_regions = {(0, 0): GATE, (0, 1): GATE + 1024, (1, 0): GATE + 2048, (1, 1): GATE + 1024, (2, 0): GATE + 1024, (2, 1): CODES0 + 512, (3, 0): RAW21, (3, 1): CODES0 + 1024}
        w1_bf = {(c, o): tile([P, P, 4], BF16, "w1_bf%d%d" % (c, o), bf_regions.get((c, o))) for c in range(4) for o in range(2)}
        w1_codes = [tile([P, 2 * P], U32, "w1_codes%d" % c, CODES0 if c == 0 else None) for c in range(4)]
        w1_scales = [tile([P, 2 * P], U8, "w1_scales%d" % c) for c in range(4)]

        def round_w1(c, o, copy):
            copy(
                w1_bf[c, o][:].rearrange("p (c n) j -> p c j n", n=4),
                w1_raw[c, o].rearrange("p j (c n) -> p c j n", n=4),
            )

        def quantise_w1(c, o):
            m = slice(P * o, P * (o + 1))
            nc.vector.quantize_mx(w1_codes[c][:, m].bitcast(FP8X4), w1_scales[c][:, m], w1_bf[c, o][:].rearrange("p c j -> p (c j)"))

        f = [tile([P, S], F32, "f%d" % c, (None, RAW21 + 1024, None, F3)[c]) for c in range(4)]

        def multiply_w1(c, o, cols, bank):
            acc = banks[bank][:, 0 : cols.stop - cols.start]
            m = slice(P * o, P * (o + 1))
            nc.tensor.matmul_mx(acc, w1_codes[c][:, m].bitcast(FP8X4), w1_scales[c][:, m], xw[o][:, cols].bitcast(FP8X4), xs[4 * o : P, cols], start=(o == 0), stop=(o == 1))

        def copy_f(c, cols, bank):
            nc.scalar.copy(f[c][:, cols], banks[bank][:, 0 : cols.stop - cols.start])

        def project(c, cols, bank):
            for o in range(2):
                multiply_w1(c, o, cols, bank)
            copy_f(c, cols, bank)

        terms = {}

        def interpolate(c, h0, halves, corners=(0, 1)):
            cols = slice(P * h0, P * (h0 + halves))
            for d in corners:
                term = tile([P, P * halves], F32, "term%d%d%d" % (c, h0, d), {(1, 0, 1): RAW30, (1, 1, 1): RAW31}.get((c, h0, d)))
                window = f[c][:].indirect(pos_sb[d][:, cols.start // 16 : cols.stop // 16])
                nc.vector.tensor_tensor(term[:], window, neg_gate[:, d, cols], MULT)
                for b in range(halves):
                    terms[c, h0 + b, d] = term[:, P * b : P * (b + 1)]

        def fetch(c, h0, halves):
            cols = slice(P * h0, P * (h0 + halves))
            picked = tile([P, P * halves], F32, "picked%d%d" % (c, h0))
            nc.scalar.activation(picked[:], f[c][:].indirect(pos_sb[1][:, cols.start // 16 : cols.stop // 16]), ACT.Copy)
            return picked

        def weigh(c, h0, halves, picked):
            term = tile([P, P * halves], F32, "term%d%d1" % (c, h0))
            nc.vector.tensor_tensor(term[:], picked[:], neg_gate[:, 1, P * h0 : P * (h0 + halves)], MULT)
            for b in range(halves):
                terms[c, h0 + b, 1] = term[:, P * b : P * (b + 1)]

        z_t = [tile([P, H], BF16, "z_t%d" % h) for h in range(2)]

        def add_turned(part, bank, b, start=False, stop=False):
            nc.tensor.matmul(banks[bank][:, P * b : P * (b + 1)], part, ident[:], start=start, stop=stop, is_transpose=True)

        def ref_part(c, h):
            return ref_sb[:, c, P * h : P * (h + 1)]

        def absolute(c0, chunks, h, bank, b0=0):
            e_t = banks[bank][:, b0 * P : (b0 + chunks) * P]
            nc.scalar.activation(
                z_t[h][:].rearrange("v (u p e) -> v u p e", u=2, e=2)[:, :, 32 * c0 : 32 * (c0 + chunks), :],
                e_t.rearrange("v (q u e) -> v u q e", u=2, e=2),
                ACT.Abs,
            )

        z_q = {}

        def quantise_z(h, copy, bank):
            words = z_t[h][:].bitcast(F32)
            z_words = banks[bank][:, 0 : 2 * P].rearrange("p (u v) -> p u v", u=2)
            for u in range(2):
                nc.tensor.transpose(z_words[:, u, :], words[:, P * u : P * (u + 1)], ident[:])
            z_bf = tile([P, 4 * P], BF16, "z_bf%d" % h)
            copy(z_bf[:].bitcast(F32).rearrange("p (v u) -> p v u", u=2), z_words.rearrange("p u v -> p v u"))
            z_codes = tile([P, P], U32, "z_codes%d" % h)
            z_scales = tile([P, P], U8, "z_scales%d" % h)
            nc.vector.quantize_mx(z_codes[:].bitcast(FP8X4), z_scales[:], z_bf[:])
            z_q[h] = (z_codes, z_scales)

        w2_codes = tile([P, N], U32, "w2_codes")
        w2_scales = tile([P, N], U8, "w2_scales")
        w2_bf = [tile([P, 2 * P, 4], BF16, "w2_bf%d" % a, F3 - 1024 + 2048 * a) for a in range(2)]

        def round_w2(a):
            dealt = w2_raw[:].rearrange("p j (r t) -> p r j t", t=4)
            nc.vector.tensor_copy(w2_bf[a][:].rearrange("p (t r) j -> p r j t", t=2), dealt[:, :, :, 2 * a : 2 * a + 2])

        def quantise_w2(t0, slots):
            m = slice(P * t0, P * (t0 + slots))
            rounded = w2_bf[t0 // 2][:, P * (t0 % 2) : P * (t0 % 2 + slots), :]
            nc.vector.quantize_mx(w2_codes[:, m].bitcast(FP8X4), w2_scales[:, m], rounded.rearrange("p r j -> p (r j)"))

        out_rows = out_0.rearrange("(r t) v -> r t v", t=4)
        out_words = out_1[0].rearrange("r c t -> r (c t)").bitcast(I32)
        y_scales = tile([P, V], U8, "y_scales")

        def multiply_w2(h, t, acc):
            z_codes, z_scales = z_q[h]
            m = slice(P * t, P * (t + 1))
            nc.tensor.matmul_mx(acc, w2_codes[:, m].bitcast(FP8X4), w2_scales[:, m], z_codes[:].bitcast(FP8X4), z_scales[:], start=True, stop=True)

        def quantise_y(h, y_bf):
            cols = slice(P * h, P * (h + 1))
            y_codes = tile([P, P], U32, "y_codes%d" % h)
            nc.vector.quantize_mx(y_codes[:].bitcast(FP8X4), y_scales[:, cols], y_bf[:].rearrange("r v t -> r (v t)"))
            nc.sync.dma_start(out_words[:, cols], y_codes[:].bitcast(I32))

        y = [tile([P, 4, P], F32, "y%d" % h) for h in range(2)]
        y_bf = [tile([P, P, 4], BF16, "y_bf%d" % h) for h in range(2)]

        def project_z(h, parts):
            for slots, bank, copy in parts:
                acc = banks[bank][:, 0 : len(slots) * P].rearrange("r (t v) -> r t v", v=P)
                for n, t in enumerate(slots):
                    multiply_w2(h, t, acc[:, n, :])
                copy(y[h][:, slots.start : slots.stop, :], acc)
            nc.sync.dma_start(out_rows[:, :, P * h : P * (h + 1)], y[h][:])

        def round_y(h, slots):
            nc.vector.tensor_copy(
                y_bf[h][:].rearrange("r (c n) t -> r c t n", n=4)[:, :, slots, :],
                y[h][:].rearrange("r t (c n) -> r c t n", n=4)[:, :, slots, :],
            )

        left, right, whole = slice(0, S // 2), slice(S // 2, S), slice(0, S)
        act, dve = nc.scalar.copy, nc.vector.tensor_copy
        pick_words(0, whole)
        nc.vector.tensor_copy(xs[:], xs_all[:].indirect(offs_sb[:]))
        pick_words(1, whole)
        round_w1(0, 0, act)
        round_w1(0, 1, act)
        quantise_w1(0, 0)
        round_w1(1, 0, act)
        quantise_w1(0, 1)
        round_w1(1, 1, dve)
        quantise_w1(1, 0)
        quantise_w1(1, 1)
        project(0, left, 0)
        project(0, right, 1)
        round_w1(2, 0, dve)
        round_w1(2, 1, act)
        project(1, whole, 2)
        interpolate(0, 0, 2, (0,))
        quantise_w1(2, 0)
        interpolate(0, 0, 2, (1,))
        quantise_w1(2, 1)
        round_w1(3, 0, act)
        round_w1(3, 1, act)
        project(2, whole, 3)
        for d in range(2):
            for h in range(2):
                add_turned(terms[0, h, d], 4, 2 * h, start=(d == 0 and h == 0))
        interpolate(1, 0, 2, (0,))
        quantise_w1(3, 0)
        multiply_w1(3, 0, left, 0)
        multiply_w1(3, 0, right, 1)
        interpolate(1, 0, 1, (1,))
        quantise_w1(3, 1)
        multiply_w1(3, 1, left, 0)
        multiply_w1(3, 1, right, 1)
        interpolate(1, 1, 1, (1,))
        picked2 = fetch(2, 1, 1)
        copy_f(3, left, 0)
        copy_f(3, right, 1)
        picked = [fetch(3, h, 1) for h in range(2)]
        for d in (1, 0):
            for h in (1, 0):
                add_turned(terms[1, h, d], 4, 2 * h + 1)
        for h in range(2):
            for c in range(2):
                add_turned(ref_part(c, h), 4, 2 * h + c, stop=(c == 1 and h == 1))
        for h in range(2):
            absolute(0, 2, h, 4, 2 * h)
        interpolate(2, 0, 2, (0,))
        interpolate(2, 0, 1, (1,))
        weigh(2, 1, 1, picked2)
        for h in range(2):
            add_turned(terms[2, h, 0], 2, h, start=(h == 0))
        for h in range(2):
            add_turned(ref_part(2, h), 2, h)
        for h in range(2):
            add_turned(terms[2, h, 1], 2, h, stop=(h == 1))
        for h in range(2):
            add_turned(ref_part(3, h), h, 0, start=True)
        for h in range(2):
            absolute(2, 1, h, 2, h)
        for h in range(2):
            weigh(3, h, 1, picked[h])
            interpolate(3, h, 1, (0,))
            for d in range(2):
                add_turned(terms[3, h, d], h, 0, stop=(d == 1))
            absolute(3, 1, h, h)
        for a in range(2):
            round_w2(a)
        quantise_w2(0, 2)
        quantise_w2(2, 1)
        quantise_z(0, act, 5)
        quantise_w2(3, 1)
        quantise_z(1, act, 6)
        project_z(0, ((range(0, 2), 3, act), (range(2, 4), 2, act)))
        project_z(1, ((range(0, 2), 7, act), (range(2, 4), 4, act)))
        round_y(0, slice(0, 4))
        round_y(1, slice(0, 2))
        round_y(1, slice(2, 4))
        for h in range(2):
            quantise_y(h, y_bf[h])
        for q in range(4):
            queue = nc.scalar if q % 2 else nc.sync
            queue.dma_start(out_2[0, 4 * q : 4 * q + 4, :].bitcast(I32), y_scales[32 * q : 32 * q + 4, :].bitcast(I32))
